import numpy as np
import ml_dtypes


def mxq(x, axis, fmt="e4m3"):
    dtype, down = {"e4m3": (ml_dtypes.float8_e4m3fn, 7), "e5m2": (ml_dtypes.float8_e5m2, 14)}[fmt]
    v = np.moveaxis(np.asarray(x, np.float32).astype(ml_dtypes.bfloat16).astype(np.float64), axis, -1)
    blocks = v.reshape(v.shape[:-1] + (-1, 32))
    amax = np.abs(blocks).max(-1, keepdims=True)
    byte = np.maximum(np.where(amax > 0, np.frexp(amax)[1] - 1 + 127, 0) - down, 1)
    scale = np.exp2(byte - 127.0)
    codes = (blocks / scale).astype(np.float32).astype(dtype).astype(np.float64)
    return np.moveaxis((codes * scale).reshape(v.shape), -1, axis)


WIDE = False


def mx_kscale(k):
    if not WIDE:
        return np.ones(k)
    levels = np.array([10, -10, 5, -5, 0])
    if k % 512:
        return np.exp2(np.random.permutation(np.resize(levels, k // 32))).repeat(32)
    a = np.empty((k // 512, 16))
    for p in range(k // 512):
        a[p, :8] = np.random.permutation(np.resize(levels, 8))
        for g in range(8):
            far = levels[np.abs(levels - a[p, g]) >= 10]
            a[p, g + 8] = far[np.random.randint(len(far))]
    return np.exp2(a.ravel()).repeat(32)


def f64(x):
    return np.asarray(x).astype(np.float64)


def striped(idx):
    return np.tile(idx.reshape(-1, 16).T, (8, 1)).astype(np.uint16)


def unstriped(offs):
    return offs[:16].T.reshape(-1).astype(np.int64)


E2M1 = np.array([0.0, 0.5, 1.0, 1.5, 2.0, 3.0, 4.0, 6.0, -0.0, -0.5, -1.0, -1.5, -2.0, -3.0, -4.0, -6.0])


def pack_weight(w, fmt):
    k, n = w.shape
    w = f64(np.asarray(w, np.float32).astype(ml_dtypes.bfloat16)).reshape(k // 32, 32, n)
    amax = np.abs(w).max(1)
    if fmt == "e4m3":
        byte = np.frexp(amax)[1] - 1 + 127 - 7
    else:
        mant, ex = np.frexp(amax / 6.0)
        byte = np.where(mant > 0.5, ex, ex - 1) + 127
    byte = np.clip(np.where(amax > 0, byte, 1), 1, 254)
    scaled = (w * np.exp2(127.0 - byte)[:, None, :]).reshape(k, n).astype(np.float32)
    by_word = np.ascontiguousarray(scaled.reshape(k // 512, 128, 4, n).transpose(0, 1, 3, 2))
    if fmt == "e4m3":
        words = by_word.astype(ml_dtypes.float8_e4m3fn).view(np.uint8)
    else:
        c = by_word.astype(ml_dtypes.float4_e2m1fn).view(np.uint8) & 0xF
        words = (c[..., 0::2] | (c[..., 1::2] << 4)).reshape(k // 512, 128, 2 * n)
    return np.ascontiguousarray(words), np.ascontiguousarray(byte.astype(np.uint8).reshape(k // 512, 16, n))


def unpack_weight(words, scales, fmt):
    g, _, n = scales.shape
    words = np.ascontiguousarray(words).reshape(g, 128, n, -1)
    if fmt == "e4m3":
        vals = words.view(ml_dtypes.float8_e4m3fn).astype(np.float64)
    else:
        nib = np.empty((g, 128, n, 4), np.uint8)
        nib[..., 0::2] = words & 0xF
        nib[..., 1::2] = words >> 4
        vals = E2M1[nib]
    vals = vals * np.repeat(np.exp2(scales.astype(np.float64) - 127.0), 8, axis=1)[..., None]
    return vals.transpose(0, 1, 3, 2).reshape(g * 512, n)


def gelu(v):
    return 0.5 * v * (1.0 + np.tanh(np.sqrt(2.0 / np.pi) * (v + 0.044715 * v**3)))


K, H, N, T, S, P = 512, 1024, 512, 2048, 1024, 512


def setup_inputs():
    n = np.random.standard_normal
    s = mx_kscale(K)[:, None]
    u = mx_kscale(H)[:, None]
    tab_words, tab_scales = pack_weight(n((K, T)) * s, "e4m3")
    w3_words, w3_scales = pack_weight(0.45 * n((K, H)) / np.sqrt(K) / s, "e2m1")
    w4_words, w4_scales = pack_weight(n((H, N)) / np.sqrt(H) / u, "e4m3")
    perm = np.random.permutation(S)
    return {
        "tab_words": tab_words, "tab_scales": tab_scales,
        "offs": striped(np.random.permutation(T)[:S]),
        "pos1": striped(perm[:P]),
        "pos2": striped(perm[P:]),
        "w1": (0.6 * n((K, H)) / np.sqrt(K) / s).astype(np.float32),
        "w2": (0.6 * n((K, H)) / np.sqrt(K) / s).astype(np.float32),
        "w3_words": w3_words, "w3_scales": w3_scales,
        "slope": np.random.uniform(0.6, 3.0, H).astype(np.float32),
        "thr": n(H).astype(np.float32),
        "pat": (1.5 * n((H, P))).astype(np.float32),
        "skip": np.random.uniform(0.6, 1.6, H).astype(np.float32),
        "wgs": np.exp(0.3 * n((128, P))).astype(np.float32),
        "gain": (np.random.uniform(0.6, 2.0, H) * u[:, 0]).astype(np.float32),
        "w4_words": w4_words, "w4_scales": w4_scales,
        "beta": (0.5 * n(N)).astype(np.float32),
    }


def reference(tab_words, tab_scales, offs, pos1, pos2, w1, w2, w3_words, w3_scales,
              slope, thr, pat, skip, wgs, gain, w4_words, w4_scales, beta):
    v = unpack_weight(tab_words, tab_scales, "e4m3")[:, unstriped(offs)]
    w3 = unpack_weight(w3_words, w3_scales, "e2m1")
    w4 = unpack_weight(w4_words, w4_scales, "e4m3")
    thin = mxq(f64(w1), 0, "e4m3").T @ v
    thick = mxq(f64(w2), 0, "e4m3").T @ v
    h = np.maximum(thin, thick) + (w3.T @ v)
    look = 1.0 / (1.0 + np.exp(-(f64(slope)[:, None] * h[:, unstriped(pos1)] + f64(thr)[:, None])))
    a = look * f64(pat)
    page = f64(skip)[:, None] * h
    page[:, unstriped(pos2)] = np.tile(f64(wgs), (H // 128, 1)) * a
    q = mxq(f64(gain)[:, None] * page, 0, "e4m3")
    return (w4.T @ q) + f64(beta)[:, None]

@@ -1,0 +1,346 @@
+from contextlib import ExitStack
+
+import concourse.mybir as mybir
+
+K, H, N, T, S, P = 512, 1024, 512, 2048, 1024, 512
+FLOPS = 2 * K * H * S * 3 + 2 * H * N * S
+
+F32 = mybir.dt.float32
+BF16 = mybir.dt.bfloat16
+I32 = mybir.dt.int32
+U32 = mybir.dt.uint32
+U16 = mybir.dt.uint16
+U8 = mybir.dt.uint8
+FP8X4 = mybir.dt.float8_e4m3fn_x4
+FP4X4 = mybir.dt.float4_e2m1fn_x4
+ALU = mybir.AluOpType
+ACT = mybir.ActivationFunctionType
+
+PART = 128
+PACK = 4
+PASS = PART * PACK
+GROUPS = H // PASS
+SLICES = GROUPS * PACK
+BANK = 512
+HALVES = S // BANK
+QUARTER = 256
+THIRD_TWICE = (5, 6, 7)
+SCALAR_CAST_SHARE = 40
+PAGE_CHUNK = (512, 256)
+SKIP_ON_SCALAR = (0, 1, 2, 3, 4, 5, 6, 7)
+
+
+def tile_list_yarn_evenness_page_kernel(
+    tc, tab_words, tab_scales, offs, pos1, pos2, w1, w2, w3_words, w3_scales,
+    slope, thr, pat, skip, wgs, gain, w4_words, w4_scales, beta, out,
+):
+    nc = tc.nc
+    with ExitStack() as ctx:
+        keep = ctx.enter_context(tc.tile_pool(name="keep", bufs=1))
+        psum = ctx.enter_context(tc.psum_pool(name="psum", bufs=1))
+        banks = [psum.tile([PART, BANK], F32, name="bank%d" % n) for n in range(8)]
+
+        def load_scale_rows(queue, plane, rows):
+            for quad in range(4):
+                queue.dma_start(
+                    out=plane[32 * quad : 32 * quad + 4].bitcast(I32),
+                    in_=rows[:, 4 * quad : 4 * quad + 4, :].rearrange("a q c -> q a c").bitcast(I32),
+                )
+
+        offs_sb = keep.tile([PART, S // 16], U16, name="offs_sb")
+        nc.sync.dma_start(offs_sb[:], offs)
+        pos1_sb = keep.tile([PART, P // 16], U16, name="pos1_sb")
+        nc.sync.dma_start(pos1_sb[:], pos1)
+        pos2_sb = keep.tile([PART, P // 16], U16, name="pos2_sb")
+        nc.sync.dma_start(pos2_sb[:], pos2)
+        w3_raw = keep.tile([PART, 2 * H], U8, name="w3_raw", align_bytes=64)
+        nc.sync.dma_start(out=w3_raw[:].bitcast(I32), in_=w3_words[0].bitcast(I32))
+        tab_sb = keep.tile([PART, T], U32, name="tab_sb", align_bytes=64)
+        nc.sync.dma_start(
+            out=tab_sb[:].bitcast(I32), in_=tab_words[0].rearrange("p t i -> p (t i)").bitcast(I32)
+        )
+        w3_raw_plane = keep.tile([PART, 1, H], U8, name="w3_raw_plane", align_bytes=64)
+        nc.gpsimd.memset(w3_raw_plane[:].bitcast(I32), 0)
+        tab_plane = keep.tile([PART, T], U8, name="tab_plane", align_bytes=64)
+        nc.vector.memset(tab_plane[:].bitcast(I32), 0)
+        for quad in range(4):
+            nc.sync.dma_start(
+                out=tab_plane[32 * quad : 32 * quad + 4, :].bitcast(I32),
+                in_=tab_scales[0, 4 * quad : 4 * quad + 4, :].bitcast(I32),
+            )
+
+        def load_rows_vector(vec, name):
+            cols = keep.tile([PART, GROUPS, PACK], F32, name=name)
+            nc.gpsimd.dma_start(out=cols[:], in_=vec.rearrange("(b p t) -> p b t", p=PART, t=PACK))
+            return cols[:].rearrange("p b t -> p (b t)")
+
+        slope_sb = load_rows_vector(slope, "slope_sb")
+        thr_sb = load_rows_vector(thr, "thr_sb")
+        skip_sb = load_rows_vector(skip, "skip_sb")
+        gain_sb = load_rows_vector(gain, "gain_sb")
+        beta_sb = keep.tile([PART, N // PART], F32, name="beta_sb")
+        with nc.allow_non_contiguous_dma(reason="one bias value a partition"):
+            nc.gpsimd.dma_start(out=beta_sb[:], in_=beta.rearrange("(c p) -> p c", p=PART))
+
+        def load_weight(w, b, name):
+            raw = keep.tile([PART, PACK, PASS], F32, name=name)
+            nc.sync.dma_start(
+                out=raw[:], in_=w.rearrange("(p j) c -> p j c", j=PACK)[:, :, b * PASS : (b + 1) * PASS]
+            )
+            return raw
+
+        def load_pat(s):
+            b, t = divmod(s, PACK)
+            rows = keep.tile([PART, P], F32, name="pat%d" % s)
+            nc.sync.dma_start(
+                out=rows[:], in_=pat.rearrange("(b p t) m -> p b t m", p=PART, t=PACK)[:, b, t, :]
+            )
+            return rows
+
+        raw = {}
+        raw[1, 0] = load_weight(w1, 0, "w1_raw0")
+        raw[2, 0] = load_weight(w2, 0, "w2_raw0")
+        load_scale_rows(nc.sync, w3_raw_plane, w3_scales)
+        wgs_sb = keep.tile([PART, PACK, P], F32, name="wgs_sb")
+        for quad in range(4):
+            nc.sync.dma_start(
+                out=wgs_sb[32 * quad : 32 * quad + 32], in_=wgs.rearrange("(p t) m -> p t m", t=PACK)
+            )
+        pat_sb = [load_pat(s) for s in range(2)]
+        raw[1, 1] = load_weight(w1, 1, "w1_raw1")
+        pat_sb.extend(load_pat(s) for s in range(2, 4))
+        raw[2, 1] = load_weight(w2, 1, "w2_raw1")
+        pat_sb.extend(load_pat(s) for s in range(4, SLICES))
+        w4_sb = keep.tile([PART, GROUPS, N], U32, name="w4_sb", align_bytes=64)
+        nc.sync.dma_start(
+            out=w4_sb[:].bitcast(I32), in_=w4_words.rearrange("a p c i -> p a (c i)").bitcast(I32)
+        )
+        w4_plane = keep.tile([PART, GROUPS, N], U8, name="w4_plane", align_bytes=64)
+        nc.gpsimd.memset(w4_plane[:].bitcast(I32), 0)
+        load_scale_rows(nc.sync, w4_plane, w4_scales)
+
+        w3_codes = keep.tile([PART, 2 * H], U8, name="w3_codes", align_bytes=64)
+        w3_plane = keep.tile([PART, H], U8, name="w3_plane", align_bytes=64)
+        for b in range(GROUPS):
+            nc.vector.tensor_copy(
+                out=w3_codes[:, 2 * PASS * b : 2 * PASS * (b + 1)].rearrange("p (t m e) -> p m t e", t=PACK, e=2),
+                in_=w3_raw[:, 2 * PASS * b : 2 * PASS * (b + 1)].rearrange("p (m t e) -> p m t e", t=PACK, e=2),
+            )
+
+        v_codes, v_plane = [], []
+        for half in range(HALVES):
+            picks = offs_sb[:, half * BANK // 16 : (half + 1) * BANK // 16]
+            words = keep.tile([PART, BANK], U32, name="v_codes%d" % half, align_bytes=64)
+            nc.vector.tensor_copy(out=words[:], in_=tab_sb[:].indirect(picks))
+            plane = keep.tile([PART, BANK], U8, name="v_plane%d" % half, align_bytes=64)
+            nc.vector.tensor_copy(out=plane[:], in_=tab_plane[:].indirect(picks))
+            v_codes.append(words)
+            v_plane.append(plane)
+
+        w_codes, w_plane = {}, {}
+
+        def round_weight(key, shares, tag):
+            grouped = keep.tile([PART, PACK, PART, PACK], BF16, name="w%d_grouped%d" % key, tag=tag, align_bytes=64)
+            dealt = grouped[:].rearrange("p t m j -> p m j t")
+            source = raw[key][:].rearrange("p j (m t) -> p m j t", t=PACK)
+            for copy, m0, m1 in shares:
+                copy(out=dealt[:, m0:m1], in_=source[:, m0:m1])
+            return grouped
+
+        def quantise_weight(key, grouped, cuts):
+            w_codes[key] = keep.tile([PART, PASS], U32, name="w%d_codes%d" % key, align_bytes=64)
+            w_plane[key] = keep.tile([PART, PASS], U8, name="w%d_plane%d" % key, align_bytes=64)
+            flat = grouped[:].rearrange("p t m j -> p (t m j)")
+            for t0, t1 in cuts:
+                nc.vector.quantize_mx(
+                    out=w_codes[key][:, t0 * PART : t1 * PART].bitcast(FP8X4),
+                    scales=w_plane[key][:, t0 * PART : t1 * PART],
+                    in_=flat[:, t0 * PASS : t1 * PASS],
+                )
+
+        on_scalar = [(nc.scalar.copy, 0, PART // 2), (nc.scalar.copy, PART // 2, PART)]
+        quantise_weight((1, 0), round_weight((1, 0), on_scalar, "w1_grouped0"), [(0, PACK)])
+        shared = [(nc.scalar.copy, 0, SCALAR_CAST_SHARE), (nc.vector.tensor_copy, SCALAR_CAST_SHARE, PART)]
+        quantise_weight((2, 0), round_weight((2, 0), shared, "w2_grouped0"), [(0, 1), (1, PACK)])
+
+        for b in range(GROUPS):
+            nc.vector.tensor_copy(
+                out=w3_plane[:, PASS * b : PASS * (b + 1)].rearrange("p (t m) -> p m t", t=PACK),
+                in_=w3_raw_plane[:, 0, PASS * b : PASS * (b + 1)].rearrange("p (m t) -> p m t", t=PACK),
+            )
+
+        def stationary(which, s):
+            b, t = divmod(s, PACK)
+            if which == 3:
+                return (
+                    w3_codes[:, 2 * PART * s : 2 * PART * (s + 1)].bitcast(FP4X4),
+                    w3_plane[:, PART * s : PART * (s + 1)],
+                )
+            cols = slice(PART * t, PART * (t + 1))
+            return w_codes[which, b][:, cols].bitcast(FP8X4), w_plane[which, b][:, cols]
+
+        def ring(name, count, width):
+            return [keep.tile([PART, width], F32, name="%s%d" % (name, n), align_bytes=64) for n in range(count)]
+
+        thin_ring, larger_ring, h_ring = ring("thin", 2, S), ring("larger", 1, S), ring("h", 2, S)
+        look_ring, factor_ring, page_ring = ring("look", 2, P), ring("factor", 2, P), ring("page", 3, S)
+        early_look = ring("early_look", 2, P)
+        taken = []
+
+        def take_bank():
+            taken.append(banks[len(taken) % len(banks)])
+            return taken[-1]
+
+        def product(s, half, weights):
+            bank = take_bank()
+            for n, which in enumerate(weights):
+                codes, plane = stationary(which, s)
+                nc.tensor.matmul_mx(
+                    out=bank[:], lhsT=codes, lhsT_scale=plane,
+                    rhs=v_codes[half][:].bitcast(FP8X4), rhs_scale=v_plane[half][:],
+                    start=(n == 0), stop=(n == len(weights) - 1),
+                )
+            return bank
+
+        cols = [slice(half * BANK, (half + 1) * BANK) for half in range(HALVES)]
+
+        def first_response(s):
+            for half in range(HALVES):
+                bank = product(s, half, (1, 3) if s in THIRD_TWICE else (1,))
+                nc.scalar.copy(out=thin_ring[s % 2][:, cols[half]], in_=bank[:])
+
+        def features(s):
+            twice = s in THIRD_TWICE
+            thin = thin_ring[s % 2]
+            h = h_ring[s % 2]
+            larger = h if twice else larger_ring[0]
+            for half in range(HALVES):
+                bank = product(s, half, (2, 3) if twice else (2,))
+                nc.vector.tensor_tensor(
+                    out=larger[:, cols[half]], in0=bank[:], in1=thin[:, cols[half]], op=ALU.max
+                )
+            if not twice:
+                for half in range(HALVES):
+                    bank = product(s, half, (3,))
+                    nc.vector.tensor_tensor(
+                        out=h[:, cols[half]], in0=bank[:], in1=larger[:, cols[half]], op=ALU.add
+                    )
+            return h
+
+        def look_and_page(s, h):
+            look = early_look[s] if s < 2 else look_ring[s % 2]
+            nc.scalar.activation(
+                out=look[:], in_=h[:].indirect(pos1_sb[:]), func=ACT.Sigmoid,
+                bias=thr_sb[:, s : s + 1], scale=slope_sb[:, s : s + 1],
+            )
+            page = page_ring[s % 3]
+            if s in SKIP_ON_SCALAR:
+                nc.scalar.activation(out=page[:], in_=h[:], func=ACT.Copy, scale=skip_sb[:, s : s + 1])
+            else:
+                nc.gpsimd.tensor_scalar(
+                    out=page[:], in0=h[:], scalar1=skip_sb[:, s : s + 1], scalar2=0.0,
+                    op0=ALU.mult, op1=ALU.add,
+                )
+            factor = factor_ring[s % 2]
+            nc.gpsimd.tensor_tensor(
+                out=factor[:], in0=pat_sb[s][:], in1=wgs_sb[:, s % PACK, :], op=ALU.mult
+            )
+            return look, factor, page
+
+        def write_page(look, factor, page):
+            nc.vector.tensor_tensor(out=page[:].indirect(pos2_sb[:]), in0=look[:], in1=factor[:], op=ALU.mult)
+
+        pairs = {}
+
+        def round_page(s, page):
+            b, t = divmod(s, PACK)
+            width = PAGE_CHUNK[b]
+            for c in range(S // width):
+                if t == 0:
+                    pairs[b, c] = keep.tile([PART, 2, width, 2], BF16, name="pairs%d_%d" % (b, c))
+                nc.scalar.activation(
+                    out=pairs[b, c][:, t // 2, :, t % 2], in_=page[:, c * width : (c + 1) * width],
+                    func=ACT.Copy, scale=gain_sb[:, s : s + 1],
+                )
+
+        q_codes, q_plane = {}, {}
+
+        q_grouped = {}
+
+        def interleave_page(b, c, copy):
+            width = PAGE_CHUNK[b]
+            grouped = keep.tile([PART, PACK * width], BF16, name="q_grouped%d_%d" % (b, c), align_bytes=64)
+            copy(
+                out=grouped[:].bitcast(F32).rearrange("p (j u) -> p j u", u=2),
+                in_=pairs[b, c][:].rearrange("p u j e -> p (u j e)").bitcast(F32).rearrange("p (u j) -> p j u", u=2),
+            )
+            q_grouped[b, c] = grouped
+
+        def quantise_page(b, c):
+            width, grouped = PAGE_CHUNK[b], q_grouped[b, c]
+            name = "q_codes%d_%d" % (b, c)
+            tag = ("factor0", "look0")[c] if b == 0 else name
+            codes = keep.tile([PART, width], U32, name=name, tag=tag, align_bytes=64)
+            plane = keep.tile([PART, width], U8, name="q_plane%d_%d" % (b, c), align_bytes=64)
+            nc.vector.quantize_mx(out=codes[:].bitcast(FP8X4), scales=plane[:], in_=grouped[:])
+            for k in range(width // QUARTER):
+                quarter = c * (width // QUARTER) + k
+                q_codes[b, quarter] = codes[:, k * QUARTER : (k + 1) * QUARTER]
+                q_plane[b, quarter] = plane[:, k * QUARTER : (k + 1) * QUARTER]
+
+        made = {}
+        first_response(0)
+        for step in range(SLICES + 2):
+            if step < SLICES:
+                h = features(step)
+                if step + 1 < SLICES:
+                    first_response(step + 1)
+                made[step] = look_and_page(step, h)
+            if 1 <= step <= SLICES:
+                write_page(*made[step - 1])
+            if step >= 2:
+                round_page(step - 2, made[step - 2][2])
+            if step in (1, 2):
+                quantise_weight((step, 1), round_weight((step, 1), on_scalar, "early_look%d" % (step - 1)), [(0, PACK)])
+            if step == PACK + 2:
+                for c in range(S // PAGE_CHUNK[0]):
+                    interleave_page(0, c, nc.scalar.copy)
+            if step == SLICES - 1:
+                for c in range(S // PAGE_CHUNK[0]):
+                    quantise_page(0, c)
+
+        def reading_pass(bank, c, quarter, b):
+            rows = slice(c * PART, (c + 1) * PART)
+            k = quarter % 2
+            nc.tensor.matmul_mx(
+                out=bank[:, k * QUARTER : (k + 1) * QUARTER],
+                lhsT=w4_sb[:, b, rows].bitcast(FP8X4), lhsT_scale=w4_plane[:, b, rows],
+                rhs=q_codes[b, quarter].bitcast(FP8X4), rhs_scale=q_plane[b, quarter],
+                start=(b == 0 and k == 0), stop=(b == GROUPS - 1 and k == 1),
+            )
+
+        sums = {}
+        for half in range(HALVES):
+            for c in range(N // PART):
+                sums[half, c] = take_bank()
+                for k in range(2):
+                    reading_pass(sums[half, c], c, 2 * half + k, 0)
+        for quarter in range(S // QUARTER):
+            interleave_page(1, quarter, nc.vector.tensor_copy)
+            quantise_page(1, quarter)
+            half = quarter // 2
+            for c in range(N // PART):
+                reading_pass(sums[half, c], c, quarter, 1)
+        for half in range(HALVES):
+            for c in range(N // PART):
+                scores = keep.tile([PART, BANK], F32, name="scores%d_%d" % (half, c))
+                bias = beta_sb[:, c : c + 1]
+                if half == 1 and c < 3:
+                    nc.vector.tensor_scalar(
+                        out=scores[:], in0=sums[half, c][:], scalar1=bias, scalar2=None, op0=ALU.add
+                    )
+                else:
+                    nc.scalar.activation(out=scores[:], in_=sums[half, c][:], func=ACT.Identity, bias=bias)
+                nc.sync.dma_start(
+                    out=out[c * PART : (c + 1) * PART, half * BANK : (half + 1) * BANK], in_=scores[:]
+                )

@@ -24,10 +24,13 @@ SLICES = GROUPS * PACK
 BANK = 512
 HALVES = S // BANK
 QUARTER = 256
-THIRD_TWICE = (5, 6, 7)
+ON_VECTOR = ((2, 1), (3, 1))
+SLOTS = 4
+LAG = 2
+THIRD_TWICE = (4, 5, 7)
 SCALAR_CAST_SHARE = 40
 PAGE_CHUNK = (512, 256)
-SKIP_ON_SCALAR = (0, 1, 2, 3, 4, 5, 6, 7)
+SKIP_ON_SCALAR = (3, 4, 7)
 
 
 def tile_list_yarn_evenness_page_kernel(
@@ -71,16 +74,9 @@ def tile_list_yarn_evenness_page_kernel(
 
         def load_rows_vector(vec, name):
             cols = keep.tile([PART, GROUPS, PACK], F32, name=name)
-            nc.gpsimd.dma_start(out=cols[:], in_=vec.rearrange("(b p t) -> p b t", p=PART, t=PACK))
+            nc.sync.dma_start(out=cols[:], in_=vec.rearrange("(b p t) -> p b t", p=PART, t=PACK))
             return cols[:].rearrange("p b t -> p (b t)")
 
-        slope_sb = load_rows_vector(slope, "slope_sb")
-        thr_sb = load_rows_vector(thr, "thr_sb")
-        skip_sb = load_rows_vector(skip, "skip_sb")
-        gain_sb = load_rows_vector(gain, "gain_sb")
-        beta_sb = keep.tile([PART, N // PART], F32, name="beta_sb")
-        with nc.allow_non_contiguous_dma(reason="one bias value a partition"):
-            nc.gpsimd.dma_start(out=beta_sb[:], in_=beta.rearrange("(c p) -> p c", p=PART))
 
         def load_weight(w, b, name):
             raw = keep.tile([PART, PACK, PASS], F32, name=name)
@@ -91,7 +87,7 @@ def tile_list_yarn_evenness_page_kernel(
 
         def load_pat(s):
             b, t = divmod(s, PACK)
-            rows = keep.tile([PART, P], F32, name="pat%d" % s)
+            rows = keep.tile([PART, P], F32, name="pat%d" % s, align_bytes=64)
             nc.sync.dma_start(
                 out=rows[:], in_=pat.rearrange("(b p t) m -> p b t m", p=PART, t=PACK)[:, b, t, :]
             )
@@ -101,16 +97,27 @@ def tile_list_yarn_evenness_page_kernel(
         raw[1, 0] = load_weight(w1, 0, "w1_raw0")
         raw[2, 0] = load_weight(w2, 0, "w2_raw0")
         load_scale_rows(nc.sync, w3_raw_plane, w3_scales)
-        wgs_sb = keep.tile([PART, PACK, P], F32, name="wgs_sb")
-        for quad in range(4):
-            nc.sync.dma_start(
-                out=wgs_sb[32 * quad : 32 * quad + 32], in_=wgs.rearrange("(p t) m -> p t m", t=PACK)
-            )
+
+        def load_wgs(t0):
+            rows = keep.tile([PART, 2, P], F32, name="wgs%d" % t0)
+            for quad in range(4):
+                nc.sync.dma_start(
+                    out=rows[32 * quad : 32 * quad + 32],
+                    in_=wgs.rearrange("(p t) m -> p t m", t=PACK)[:, t0 : t0 + 2, :],
+                )
+            return [rows[:, 0, :], rows[:, 1, :]]
+
+        slope_sb = load_rows_vector(slope, "slope_sb")
+        thr_sb = load_rows_vector(thr, "thr_sb")
+        skip_sb = load_rows_vector(skip, "skip_sb")
+        wgs_sb = load_wgs(0)
         pat_sb = [load_pat(s) for s in range(2)]
+        wgs_sb.extend(load_wgs(2))
+        pat_sb.append(load_pat(2))
         raw[1, 1] = load_weight(w1, 1, "w1_raw1")
-        pat_sb.extend(load_pat(s) for s in range(2, 4))
+        gain_sb = load_rows_vector(gain, "gain_sb")
         raw[2, 1] = load_weight(w2, 1, "w2_raw1")
-        pat_sb.extend(load_pat(s) for s in range(4, SLICES))
+        pat_sb.extend(load_pat(s) for s in range(3, SLICES))
         w4_sb = keep.tile([PART, GROUPS, N], U32, name="w4_sb", align_bytes=64)
         nc.sync.dma_start(
             out=w4_sb[:].bitcast(I32), in_=w4_words.rearrange("a p c i -> p a (c i)").bitcast(I32)
@@ -118,13 +125,16 @@ def tile_list_yarn_evenness_page_kernel(
         w4_plane = keep.tile([PART, GROUPS, N], U8, name="w4_plane", align_bytes=64)
         nc.gpsimd.memset(w4_plane[:].bitcast(I32), 0)
         load_scale_rows(nc.sync, w4_plane, w4_scales)
+        beta_sb = keep.tile([PART, N // PART], F32, name="beta_sb")
+        with nc.allow_non_contiguous_dma(reason="one bias value a partition"):
+            nc.sync.dma_start(out=beta_sb[:], in_=beta.rearrange("(c p) -> p c", p=PART))
 
         w3_codes = keep.tile([PART, 2 * H], U8, name="w3_codes", align_bytes=64)
         w3_plane = keep.tile([PART, H], U8, name="w3_plane", align_bytes=64)
         for b in range(GROUPS):
             nc.vector.tensor_copy(
-                out=w3_codes[:, 2 * PASS * b : 2 * PASS * (b + 1)].rearrange("p (t m e) -> p m t e", t=PACK, e=2),
-                in_=w3_raw[:, 2 * PASS * b : 2 * PASS * (b + 1)].rearrange("p (m t e) -> p m t e", t=PACK, e=2),
+                out=w3_codes[:].bitcast(U16)[:, PASS * b : PASS * (b + 1)].rearrange("p (t m) -> p t m", t=PACK),
+                in_=w3_raw[:].bitcast(U16)[:, PASS * b : PASS * (b + 1)].rearrange("p (m t) -> p t m", t=PACK),
             )
 
         v_codes, v_plane = [], []
@@ -147,8 +157,8 @@ def tile_list_yarn_evenness_page_kernel(
                 copy(out=dealt[:, m0:m1], in_=source[:, m0:m1])
             return grouped
 
-        def quantise_weight(key, grouped, cuts):
-            w_codes[key] = keep.tile([PART, PASS], U32, name="w%d_codes%d" % key, align_bytes=64)
+        def quantise_weight(key, grouped, cuts, tag):
+            w_codes[key] = keep.tile([PART, PASS], U32, name="w%d_codes%d" % key, tag=tag, align_bytes=64)
             w_plane[key] = keep.tile([PART, PASS], U8, name="w%d_plane%d" % key, align_bytes=64)
             flat = grouped[:].rearrange("p t m j -> p (t m j)")
             for t0, t1 in cuts:
@@ -159,14 +169,14 @@ def tile_list_yarn_evenness_page_kernel(
                 )
 
         on_scalar = [(nc.scalar.copy, 0, PART // 2), (nc.scalar.copy, PART // 2, PART)]
-        quantise_weight((1, 0), round_weight((1, 0), on_scalar, "w1_grouped0"), [(0, PACK)])
+        quantise_weight((1, 0), round_weight((1, 0), on_scalar, "w1_grouped0"), [(0, PACK)], "w1_codes0")
         shared = [(nc.scalar.copy, 0, SCALAR_CAST_SHARE), (nc.vector.tensor_copy, SCALAR_CAST_SHARE, PART)]
-        quantise_weight((2, 0), round_weight((2, 0), shared, "w2_grouped0"), [(0, 1), (1, PACK)])
+        quantise_weight((2, 0), round_weight((2, 0), shared, "w2_grouped0"), [(0, 1), (1, PACK)], "w2_codes0")
 
         for b in range(GROUPS):
             nc.vector.tensor_copy(
-                out=w3_plane[:, PASS * b : PASS * (b + 1)].rearrange("p (t m) -> p m t", t=PACK),
-                in_=w3_raw_plane[:, 0, PASS * b : PASS * (b + 1)].rearrange("p (m t) -> p m t", t=PACK),
+                out=w3_plane[:, PASS * b : PASS * (b + 1)].rearrange("p (t m) -> p t m", t=PACK),
+                in_=w3_raw_plane[:, 0, PASS * b : PASS * (b + 1)].rearrange("p (m t) -> p t m", t=PACK),
             )
 
         def stationary(which, s):
@@ -183,8 +193,13 @@ def tile_list_yarn_evenness_page_kernel(
             return [keep.tile([PART, width], F32, name="%s%d" % (name, n), align_bytes=64) for n in range(count)]
 
         thin_ring, larger_ring, h_ring = ring("thin", 2, S), ring("larger", 1, S), ring("h", 2, S)
-        look_ring, factor_ring, page_ring = ring("look", 2, P), ring("factor", 2, P), ring("page", 3, S)
+        look_ring, factor_ring, page_ring = ring("look", 2, P), ring("factor", 3, P), ring("page", SLOTS, S)
         early_look = ring("early_look", 2, P)
+        early_thin, early_larger = ring("early_thin", 1, S)[0], ring("early_larger", 1, S)[0]
+
+        def thin_tile(s):
+            return early_thin if s == 1 else thin_ring[s % 2]
+
         taken = []
 
         def take_bank():
@@ -207,13 +222,13 @@ def tile_list_yarn_evenness_page_kernel(
         def first_response(s):
             for half in range(HALVES):
                 bank = product(s, half, (1, 3) if s in THIRD_TWICE else (1,))
-                nc.scalar.copy(out=thin_ring[s % 2][:, cols[half]], in_=bank[:])
+                nc.scalar.copy(out=thin_tile(s)[:, cols[half]], in_=bank[:])
 
         def features(s):
             twice = s in THIRD_TWICE
-            thin = thin_ring[s % 2]
+            thin = thin_tile(s)
             h = h_ring[s % 2]
-            larger = h if twice else larger_ring[0]
+            larger = h if twice else early_larger if s < 3 else larger_ring[0]
             for half in range(HALVES):
                 bank = product(s, half, (2, 3) if twice else (2,))
                 nc.vector.tensor_tensor(
@@ -233,7 +248,7 @@ def tile_list_yarn_evenness_page_kernel(
                 out=look[:], in_=h[:].indirect(pos1_sb[:]), func=ACT.Sigmoid,
                 bias=thr_sb[:, s : s + 1], scale=slope_sb[:, s : s + 1],
             )
-            page = page_ring[s % 3]
+            page = page_ring[s % SLOTS]
             if s in SKIP_ON_SCALAR:
                 nc.scalar.activation(out=page[:], in_=h[:], func=ACT.Copy, scale=skip_sb[:, s : s + 1])
             else:
@@ -241,25 +256,25 @@ def tile_list_yarn_evenness_page_kernel(
                     out=page[:], in0=h[:], scalar1=skip_sb[:, s : s + 1], scalar2=0.0,
                     op0=ALU.mult, op1=ALU.add,
                 )
-            factor = factor_ring[s % 2]
+            factor = factor_ring[s % 3]
             nc.gpsimd.tensor_tensor(
-                out=factor[:], in0=pat_sb[s][:], in1=wgs_sb[:, s % PACK, :], op=ALU.mult
+                out=factor[:], in0=pat_sb[s][:], in1=wgs_sb[s % PACK], op=ALU.mult
             )
             return look, factor, page
 
         def write_page(look, factor, page):
             nc.vector.tensor_tensor(out=page[:].indirect(pos2_sb[:]), in0=look[:], in1=factor[:], op=ALU.mult)
 
-        pairs = {}
+        rounded = {}
 
         def round_page(s, page):
             b, t = divmod(s, PACK)
             width = PAGE_CHUNK[b]
             for c in range(S // width):
                 if t == 0:
-                    pairs[b, c] = keep.tile([PART, 2, width, 2], BF16, name="pairs%d_%d" % (b, c))
+                    rounded[b, c] = keep.tile([PART, PACK, width], BF16, name="rounded%d_%d" % (b, c))
                 nc.scalar.activation(
-                    out=pairs[b, c][:, t // 2, :, t % 2], in_=page[:, c * width : (c + 1) * width],
+                    out=rounded[b, c][:, t, :], in_=page[:, c * width : (c + 1) * width],
                     func=ACT.Copy, scale=gain_sb[:, s : s + 1],
                 )
 
@@ -269,10 +284,12 @@ def tile_list_yarn_evenness_page_kernel(
 
         def interleave_page(b, c, copy):
             width = PAGE_CHUNK[b]
-            grouped = keep.tile([PART, PACK * width], BF16, name="q_grouped%d_%d" % (b, c), align_bytes=64)
+            name = "q_grouped%d_%d" % (b, c)
+            tag = "pat%d" % (SLICES - 2 + c) if b == 0 else name
+            grouped = keep.tile([PART, PACK * width], BF16, name=name, tag=tag, align_bytes=64)
             copy(
-                out=grouped[:].bitcast(F32).rearrange("p (j u) -> p j u", u=2),
-                in_=pairs[b, c][:].rearrange("p u j e -> p (u j e)").bitcast(F32).rearrange("p (u j) -> p j u", u=2),
+                out=grouped[:].rearrange("p (j i t) -> p j t i", i=PACK, t=PACK),
+                in_=rounded[b, c][:].rearrange("p t (j i) -> p j t i", i=PACK),
             )
             q_grouped[b, c] = grouped
 
@@ -290,57 +307,64 @@ def tile_list_yarn_evenness_page_kernel(
 
         made = {}
         first_response(0)
-        for step in range(SLICES + 2):
+        for step in range(SLICES + LAG):
             if step < SLICES:
                 h = features(step)
+                if step == 2:
+                    quantise_weight((1, 1), late1, [(0, PACK)], "early_larger0")
                 if step + 1 < SLICES:
                     first_response(step + 1)
                 made[step] = look_and_page(step, h)
             if 1 <= step <= SLICES:
                 write_page(*made[step - 1])
-            if step >= 2:
-                round_page(step - 2, made[step - 2][2])
-            if step in (1, 2):
-                quantise_weight((step, 1), round_weight((step, 1), on_scalar, "early_look%d" % (step - 1)), [(0, PACK)])
-            if step == PACK + 2:
+            if step >= LAG:
+                round_page(step - LAG, made[step - LAG][2])
+            if step == 1:
+                late1 = round_weight((1, 1), on_scalar, "early_thin0")
+                late2 = round_weight((2, 1), on_scalar, "early_look0")
+            if step == 2:
+                quantise_weight((2, 1), late2, [(0, PACK)], "early_look1")
+            if step == PACK - 1 + LAG:
                 for c in range(S // PAGE_CHUNK[0]):
-                    interleave_page(0, c, nc.scalar.copy)
+                    interleave_page(0, c, (nc.vector.tensor_copy, nc.scalar.copy)[c])
             if step == SLICES - 1:
                 for c in range(S // PAGE_CHUNK[0]):
                     quantise_page(0, c)
 
-        def reading_pass(bank, c, quarter, b):
-            rows = slice(c * PART, (c + 1) * PART)
-            k = quarter % 2
-            nc.tensor.matmul_mx(
-                out=bank[:, k * QUARTER : (k + 1) * QUARTER],
-                lhsT=w4_sb[:, b, rows].bitcast(FP8X4), lhsT_scale=w4_plane[:, b, rows],
-                rhs=q_codes[b, quarter].bitcast(FP8X4), rhs_scale=q_plane[b, quarter],
-                start=(b == 0 and k == 0), stop=(b == GROUPS - 1 and k == 1),
-            )
+        def reading_pass(bank, pair, quarter, b):
+            for k in range(2):
+                rows = slice((2 * pair + k) * PART, (2 * pair + k + 1) * PART)
+                nc.tensor.matmul_mx(
+                    out=bank[:, k * QUARTER : (k + 1) * QUARTER],
+                    lhsT=w4_sb[:, b, rows].bitcast(FP8X4), lhsT_scale=w4_plane[:, b, rows],
+                    rhs=q_codes[b, quarter].bitcast(FP8X4), rhs_scale=q_plane[b, quarter],
+                    start=(b == 0 and k == 0), stop=(b == GROUPS - 1 and k == 1),
+                )
 
         sums = {}
-        for half in range(HALVES):
-            for c in range(N // PART):
-                sums[half, c] = take_bank()
-                for k in range(2):
-                    reading_pass(sums[half, c], c, 2 * half + k, 0)
+        for quarter in range(S // QUARTER):
+            for pair in range(2):
+                sums[quarter, pair] = take_bank()
+                reading_pass(sums[quarter, pair], pair, quarter, 0)
         for quarter in range(S // QUARTER):
             interleave_page(1, quarter, nc.vector.tensor_copy)
             quantise_page(1, quarter)
-            half = quarter // 2
-            for c in range(N // PART):
-                reading_pass(sums[half, c], c, quarter, 1)
-        for half in range(HALVES):
-            for c in range(N // PART):
-                scores = keep.tile([PART, BANK], F32, name="scores%d_%d" % (half, c))
-                bias = beta_sb[:, c : c + 1]
-                if half == 1 and c < 3:
-                    nc.vector.tensor_scalar(
-                        out=scores[:], in0=sums[half, c][:], scalar1=bias, scalar2=None, op0=ALU.add
-                    )
-                else:
-                    nc.scalar.activation(out=scores[:], in_=sums[half, c][:], func=ACT.Identity, bias=bias)
+            for pair in range(2):
+                reading_pass(sums[quarter, pair], pair, quarter, 1)
+        out_rows = out.rearrange("(c p) j -> p c j", p=PART)
+        for quarter in range(S // QUARTER):
+            for pair in range(2):
+                scores = keep.tile([PART, 2, QUARTER], F32, name="scores%d_%d" % (quarter, pair))
+                for k in range(2):
+                    bias = beta_sb[:, 2 * pair + k : 2 * pair + k + 1]
+                    part = sums[quarter, pair][:, k * QUARTER : (k + 1) * QUARTER]
+                    if (quarter, pair) in ON_VECTOR:
+                        nc.vector.tensor_scalar(
+                            out=scores[:, k, :], in0=part, scalar1=bias, scalar2=None, op0=ALU.add
+                        )
+                    else:
+                        nc.scalar.activation(out=scores[:, k, :], in_=part, func=ACT.Identity, bias=bias)
                 nc.sync.dma_start(
-                    out=out[c * PART : (c + 1) * PART, half * BANK : (half + 1) * BANK], in_=scores[:]
+                    out=out_rows[:, 2 * pair : 2 * pair + 2, quarter * QUARTER : (quarter + 1) * QUARTER],
+                    in_=scores[:],
                 )

@@ -24,13 +24,14 @@ SLICES = GROUPS * PACK
 BANK = 512
 HALVES = S // BANK
 QUARTER = 256
+SKIP_ON_VECTOR = (0, 1, 2, 6,)
 ON_VECTOR = ((2, 1), (3, 1))
 SLOTS = 4
 LAG = 2
-THIRD_TWICE = (4, 5, 7)
-SCALAR_CAST_SHARE = 40
+THIRD_TWICE = (2, 3, 7)
+SCALAR_CAST_SHARE = 64
 PAGE_CHUNK = (512, 256)
-SKIP_ON_SCALAR = (3, 4, 7)
+SKIP_ON_SCALAR = (3, 4, 5, 7,)
 
 
 def tile_list_yarn_evenness_page_kernel(
@@ -78,12 +79,15 @@ def tile_list_yarn_evenness_page_kernel(
             return cols[:].rearrange("p b t -> p (b t)")
 
 
-        def load_weight(w, b, name):
-            raw = keep.tile([PART, PACK, PASS], F32, name=name)
-            nc.sync.dma_start(
-                out=raw[:], in_=w.rearrange("(p j) c -> p j c", j=PACK)[:, :, b * PASS : (b + 1) * PASS]
-            )
-            return raw
+        def load_weight(w, b, name, parts):
+            width = PASS // parts
+            tiles = []
+            for n in range(parts):
+                part = keep.tile([PART, PACK, width], F32, name="%s_%d" % (name, n))
+                c0 = b * PASS + n * width
+                nc.sync.dma_start(out=part[:], in_=w.rearrange("(p j) c -> p j c", j=PACK)[:, :, c0 : c0 + width])
+                tiles.append(part)
+            return tiles
 
         def load_pat(s):
             b, t = divmod(s, PACK)
@@ -94,8 +98,8 @@ def tile_list_yarn_evenness_page_kernel(
             return rows
 
         raw = {}
-        raw[1, 0] = load_weight(w1, 0, "w1_raw0")
-        raw[2, 0] = load_weight(w2, 0, "w2_raw0")
+        raw[1, 0] = load_weight(w1, 0, "w1_raw0", 2)
+        raw[2, 0] = load_weight(w2, 0, "w2_raw0", 2)
         load_scale_rows(nc.sync, w3_raw_plane, w3_scales)
 
         def load_wgs(t0):
@@ -111,12 +115,12 @@ def tile_list_yarn_evenness_page_kernel(
         thr_sb = load_rows_vector(thr, "thr_sb")
         skip_sb = load_rows_vector(skip, "skip_sb")
         wgs_sb = load_wgs(0)
-        pat_sb = [load_pat(s) for s in range(2)]
+        pat_sb = [load_pat(0), load_pat(1)]
+        raw[1, 1] = load_weight(w1, 1, "w1_raw1", 1)
+        raw[2, 1] = load_weight(w2, 1, "w2_raw1", 1)
         wgs_sb.extend(load_wgs(2))
         pat_sb.append(load_pat(2))
-        raw[1, 1] = load_weight(w1, 1, "w1_raw1")
         gain_sb = load_rows_vector(gain, "gain_sb")
-        raw[2, 1] = load_weight(w2, 1, "w2_raw1")
         pat_sb.extend(load_pat(s) for s in range(3, SLICES))
         w4_sb = keep.tile([PART, GROUPS, N], U32, name="w4_sb", align_bytes=64)
         nc.sync.dma_start(
@@ -130,7 +134,6 @@ def tile_list_yarn_evenness_page_kernel(
             nc.sync.dma_start(out=beta_sb[:], in_=beta.rearrange("(c p) -> p c", p=PART))
 
         w3_codes = keep.tile([PART, 2 * H], U8, name="w3_codes", align_bytes=64)
-        w3_plane = keep.tile([PART, H], U8, name="w3_plane", align_bytes=64)
         for b in range(GROUPS):
             nc.vector.tensor_copy(
                 out=w3_codes[:].bitcast(U16)[:, PASS * b : PASS * (b + 1)].rearrange("p (t m) -> p t m", t=PACK),
@@ -152,9 +155,10 @@ def tile_list_yarn_evenness_page_kernel(
         def round_weight(key, shares, tag):
             grouped = keep.tile([PART, PACK, PART, PACK], BF16, name="w%d_grouped%d" % key, tag=tag, align_bytes=64)
             dealt = grouped[:].rearrange("p t m j -> p m j t")
-            source = raw[key][:].rearrange("p j (m t) -> p m j t", t=PACK)
+            span = PART // len(raw[key])
             for copy, m0, m1 in shares:
-                copy(out=dealt[:, m0:m1], in_=source[:, m0:m1])
+                source = raw[key][m0 // span][:].rearrange("p j (m t) -> p m j t", t=PACK)
+                copy(out=dealt[:, m0:m1], in_=source[:, m0 % span : m0 % span + m1 - m0])
             return grouped
 
         def quantise_weight(key, grouped, cuts, tag):
@@ -173,6 +177,7 @@ def tile_list_yarn_evenness_page_kernel(
         shared = [(nc.scalar.copy, 0, SCALAR_CAST_SHARE), (nc.vector.tensor_copy, SCALAR_CAST_SHARE, PART)]
         quantise_weight((2, 0), round_weight((2, 0), shared, "w2_grouped0"), [(0, 1), (1, PACK)], "w2_codes0")
 
+        w3_plane = keep.tile([PART, H], U8, name="w3_plane", align_bytes=64)
         for b in range(GROUPS):
             nc.vector.tensor_copy(
                 out=w3_plane[:, PASS * b : PASS * (b + 1)].rearrange("p (t m) -> p t m", t=PACK),
@@ -192,13 +197,12 @@ def tile_list_yarn_evenness_page_kernel(
         def ring(name, count, width):
             return [keep.tile([PART, width], F32, name="%s%d" % (name, n), align_bytes=64) for n in range(count)]
 
-        thin_ring, larger_ring, h_ring = ring("thin", 2, S), ring("larger", 1, S), ring("h", 2, S)
-        look_ring, factor_ring, page_ring = ring("look", 2, P), ring("factor", 3, P), ring("page", SLOTS, S)
+        thin_ring, h_ring = ring("thin", 2, S), ring("h", 2, S)
+        look_ring, factor_ring, page_ring = ring("look", 2, P), ring("factor", 2, P), ring("page", SLOTS, S)
         early_look = ring("early_look", 2, P)
-        early_thin, early_larger = ring("early_thin", 1, S)[0], ring("early_larger", 1, S)[0]
 
         def thin_tile(s):
-            return early_thin if s == 1 else thin_ring[s % 2]
+            return thin_ring[min(s, 1)]
 
         taken = []
 
@@ -228,17 +232,16 @@ def tile_list_yarn_evenness_page_kernel(
             twice = s in THIRD_TWICE
             thin = thin_tile(s)
             h = h_ring[s % 2]
-            larger = h if twice else early_larger if s < 3 else larger_ring[0]
             for half in range(HALVES):
                 bank = product(s, half, (2, 3) if twice else (2,))
                 nc.vector.tensor_tensor(
-                    out=larger[:, cols[half]], in0=bank[:], in1=thin[:, cols[half]], op=ALU.max
+                    out=h[:, cols[half]], in0=bank[:], in1=thin[:, cols[half]], op=ALU.max
                 )
             if not twice:
                 for half in range(HALVES):
                     bank = product(s, half, (3,))
                     nc.vector.tensor_tensor(
-                        out=h[:, cols[half]], in0=bank[:], in1=larger[:, cols[half]], op=ALU.add
+                        out=h[:, cols[half]], in0=bank[:], in1=h[:, cols[half]], op=ALU.add
                     )
             return h
 
@@ -251,12 +254,16 @@ def tile_list_yarn_evenness_page_kernel(
             page = page_ring[s % SLOTS]
             if s in SKIP_ON_SCALAR:
                 nc.scalar.activation(out=page[:], in_=h[:], func=ACT.Copy, scale=skip_sb[:, s : s + 1])
+            elif s in SKIP_ON_VECTOR:
+                nc.vector.tensor_scalar(
+                    out=page[:], in0=h[:], scalar1=skip_sb[:, s : s + 1], scalar2=None, op0=ALU.mult
+                )
             else:
                 nc.gpsimd.tensor_scalar(
                     out=page[:], in0=h[:], scalar1=skip_sb[:, s : s + 1], scalar2=0.0,
                     op0=ALU.mult, op1=ALU.add,
                 )
-            factor = factor_ring[s % 3]
+            factor = factor_ring[s % 2]
             nc.gpsimd.tensor_tensor(
                 out=factor[:], in0=pat_sb[s][:], in1=wgs_sb[s % PACK], op=ALU.mult
             )
@@ -285,10 +292,16 @@ def tile_list_yarn_evenness_page_kernel(
         def interleave_page(b, c, copy):
             width = PAGE_CHUNK[b]
             name = "q_grouped%d_%d" % (b, c)
-            tag = "pat%d" % (SLICES - 2 + c) if b == 0 else name
-            grouped = keep.tile([PART, PACK * width], BF16, name=name, tag=tag, align_bytes=64)
+            if b == 0:
+                grouped = keep.tile([PART, PACK * width], BF16, name=name, tag=("pat6", "pat5")[c], align_bytes=64)[:]
+            elif c < 2:
+                grouped = keep.tile([PART, PACK * width], BF16, name=name, align_bytes=64)[:]
+            else:
+                if c == 2:
+                    q_grouped["rest"] = keep.tile([PART, 2 * PACK * width], BF16, name=name, tag="q_grouped1_0", align_bytes=64)
+                grouped = q_grouped["rest"][:, (c - 2) * PACK * width : (c - 1) * PACK * width]
             copy(
-                out=grouped[:].rearrange("p (j i t) -> p j t i", i=PACK, t=PACK),
+                out=grouped.rearrange("p (j i t) -> p j t i", i=PACK, t=PACK),
                 in_=rounded[b, c][:].rearrange("p t (j i) -> p j t i", i=PACK),
             )
             q_grouped[b, c] = grouped
@@ -299,7 +312,7 @@ def tile_list_yarn_evenness_page_kernel(
             tag = ("factor0", "look0")[c] if b == 0 else name
             codes = keep.tile([PART, width], U32, name=name, tag=tag, align_bytes=64)
             plane = keep.tile([PART, width], U8, name="q_plane%d_%d" % (b, c), align_bytes=64)
-            nc.vector.quantize_mx(out=codes[:].bitcast(FP8X4), scales=plane[:], in_=grouped[:])
+            nc.vector.quantize_mx(out=codes[:].bitcast(FP8X4), scales=plane[:], in_=grouped)
             for k in range(width // QUARTER):
                 quarter = c * (width // QUARTER) + k
                 q_codes[b, quarter] = codes[:, k * QUARTER : (k + 1) * QUARTER]
@@ -310,8 +323,6 @@ def tile_list_yarn_evenness_page_kernel(
         for step in range(SLICES + LAG):
             if step < SLICES:
                 h = features(step)
-                if step == 2:
-                    quantise_weight((1, 1), late1, [(0, PACK)], "early_larger0")
                 if step + 1 < SLICES:
                     first_response(step + 1)
                 made[step] = look_and_page(step, h)
@@ -320,9 +331,10 @@ def tile_list_yarn_evenness_page_kernel(
             if step >= LAG:
                 round_page(step - LAG, made[step - LAG][2])
             if step == 1:
-                late1 = round_weight((1, 1), on_scalar, "early_thin0")
+                late1 = round_weight((1, 1), on_scalar, "pat1")
                 late2 = round_weight((2, 1), on_scalar, "early_look0")
             if step == 2:
+                quantise_weight((1, 1), late1, [(0, PACK)], "pat2")
                 quantise_weight((2, 1), late2, [(0, PACK)], "early_look1")
             if step == PACK - 1 + LAG:
                 for c in range(S // PAGE_CHUNK[0]):
@@ -347,7 +359,7 @@ def tile_list_yarn_evenness_page_kernel(
                 sums[quarter, pair] = take_bank()
                 reading_pass(sums[quarter, pair], pair, quarter, 0)
         for quarter in range(S // QUARTER):
-            interleave_page(1, quarter, nc.vector.tensor_copy)
+            interleave_page(1, quarter, nc.scalar.copy if quarter == 1 else nc.vector.tensor_copy)
             quantise_page(1, quarter)
             for pair in range(2):
                 reading_pass(sums[quarter, pair], pair, quarter, 1)

@@ -24,6 +24,7 @@ SLICES = GROUPS * PACK
 BANK = 512
 HALVES = S // BANK
 QUARTER = 256
+EARLY = 3
 SKIP_ON_VECTOR = (0, 1, 2, 6,)
 ON_VECTOR = ((2, 1), (3, 1))
 SLOTS = 4
@@ -57,8 +58,6 @@ def tile_list_yarn_evenness_page_kernel(
         nc.sync.dma_start(pos1_sb[:], pos1)
         pos2_sb = keep.tile([PART, P // 16], U16, name="pos2_sb")
         nc.sync.dma_start(pos2_sb[:], pos2)
-        w3_raw = keep.tile([PART, 2 * H], U8, name="w3_raw", align_bytes=64)
-        nc.sync.dma_start(out=w3_raw[:].bitcast(I32), in_=w3_words[0].bitcast(I32))
         tab_sb = keep.tile([PART, T], U32, name="tab_sb", align_bytes=64)
         nc.sync.dma_start(
             out=tab_sb[:].bitcast(I32), in_=tab_words[0].rearrange("p t i -> p (t i)").bitcast(I32)
@@ -100,6 +99,8 @@ def tile_list_yarn_evenness_page_kernel(
         raw = {}
         raw[1, 0] = load_weight(w1, 0, "w1_raw0", 2)
         raw[2, 0] = load_weight(w2, 0, "w2_raw0", 2)
+        w3_raw = keep.tile([PART, 2 * H], U8, name="w3_raw", align_bytes=64)
+        nc.sync.dma_start(out=w3_raw[:].bitcast(I32), in_=w3_words[0].bitcast(I32))
         load_scale_rows(nc.sync, w3_raw_plane, w3_scales)
 
         def load_wgs(t0):
@@ -134,11 +135,6 @@ def tile_list_yarn_evenness_page_kernel(
             nc.sync.dma_start(out=beta_sb[:], in_=beta.rearrange("(c p) -> p c", p=PART))
 
         w3_codes = keep.tile([PART, 2 * H], U8, name="w3_codes", align_bytes=64)
-        for b in range(GROUPS):
-            nc.vector.tensor_copy(
-                out=w3_codes[:].bitcast(U16)[:, PASS * b : PASS * (b + 1)].rearrange("p (t m) -> p t m", t=PACK),
-                in_=w3_raw[:].bitcast(U16)[:, PASS * b : PASS * (b + 1)].rearrange("p (m t) -> p t m", t=PACK),
-            )
 
         v_codes, v_plane = [], []
         for half in range(HALVES):
@@ -179,6 +175,10 @@ def tile_list_yarn_evenness_page_kernel(
 
         w3_plane = keep.tile([PART, H], U8, name="w3_plane", align_bytes=64)
         for b in range(GROUPS):
+            nc.vector.tensor_copy(
+                out=w3_codes[:].bitcast(U16)[:, PASS * b : PASS * (b + 1)].rearrange("p (t m) -> p t m", t=PACK),
+                in_=w3_raw[:].bitcast(U16)[:, PASS * b : PASS * (b + 1)].rearrange("p (m t) -> p t m", t=PACK),
+            )
             nc.vector.tensor_copy(
                 out=w3_plane[:, PASS * b : PASS * (b + 1)].rearrange("p (t m) -> p t m", t=PACK),
                 in_=w3_raw_plane[:, 0, PASS * b : PASS * (b + 1)].rearrange("p (m t) -> p t m", t=PACK),
@@ -245,12 +245,8 @@ def tile_list_yarn_evenness_page_kernel(
                     )
             return h
 
-        def look_and_page(s, h):
-            look = early_look[s] if s < 2 else look_ring[s % 2]
-            nc.scalar.activation(
-                out=look[:], in_=h[:].indirect(pos1_sb[:]), func=ACT.Sigmoid,
-                bias=thr_sb[:, s : s + 1], scale=slope_sb[:, s : s + 1],
-            )
+        def fill_page(s):
+            h = h_ring[s % 2]
             page = page_ring[s % SLOTS]
             if s in SKIP_ON_SCALAR:
                 nc.scalar.activation(out=page[:], in_=h[:], func=ACT.Copy, scale=skip_sb[:, s : s + 1])
@@ -263,6 +259,16 @@ def tile_list_yarn_evenness_page_kernel(
                     out=page[:], in0=h[:], scalar1=skip_sb[:, s : s + 1], scalar2=0.0,
                     op0=ALU.mult, op1=ALU.add,
                 )
+
+        def look_and_page(s, h):
+            look = early_look[s] if s < 2 else look_ring[s % 2]
+            nc.scalar.activation(
+                out=look[:], in_=h[:].indirect(pos1_sb[:]), func=ACT.Sigmoid,
+                bias=thr_sb[:, s : s + 1], scale=slope_sb[:, s : s + 1],
+            )
+            page = page_ring[s % SLOTS]
+            if s > 0:
+                fill_page(s)
             factor = factor_ring[s % 2]
             nc.gpsimd.tensor_tensor(
                 out=factor[:], in0=pat_sb[s][:], in1=wgs_sb[s % PACK], op=ALU.mult
@@ -306,23 +312,27 @@ def tile_list_yarn_evenness_page_kernel(
             )
             q_grouped[b, c] = grouped
 
-        def quantise_page(b, c):
-            width, grouped = PAGE_CHUNK[b], q_grouped[b, c]
-            name = "q_codes%d_%d" % (b, c)
-            tag = ("factor0", "look0")[c] if b == 0 else name
-            codes = keep.tile([PART, width], U32, name=name, tag=tag, align_bytes=64)
-            plane = keep.tile([PART, width], U8, name="q_plane%d_%d" % (b, c), align_bytes=64)
-            nc.vector.quantize_mx(out=codes[:].bitcast(FP8X4), scales=plane[:], in_=grouped)
-            for k in range(width // QUARTER):
-                quarter = c * (width // QUARTER) + k
-                q_codes[b, quarter] = codes[:, k * QUARTER : (k + 1) * QUARTER]
-                q_plane[b, quarter] = plane[:, k * QUARTER : (k + 1) * QUARTER]
+        def quantise_page(b, first, count, tag):
+            name = "q%d_%d" % (b, first)
+            codes = keep.tile([PART, count * QUARTER], U32, name=name + "_codes", tag=tag, align_bytes=64)
+            plane = keep.tile([PART, count * QUARTER], U8, name=name + "_plane", align_bytes=64)
+            for k in range(count):
+                c, col = divmod((first + k) * QUARTER, PAGE_CHUNK[b])
+                cols_k = slice(k * QUARTER, (k + 1) * QUARTER)
+                q_codes[b, first + k], q_plane[b, first + k] = codes[:, cols_k], plane[:, cols_k]
+                nc.vector.quantize_mx(
+                    out=codes[:, cols_k].bitcast(FP8X4), scales=plane[:, cols_k],
+                    in_=q_grouped[b, c][:, PACK * col : PACK * (col + QUARTER)],
+                )
 
         made = {}
         first_response(0)
         for step in range(SLICES + LAG):
             if step < SLICES:
                 h = features(step)
+            if step == 1:
+                fill_page(step - 1)
+            if step < SLICES:
                 if step + 1 < SLICES:
                     first_response(step + 1)
                 made[step] = look_and_page(step, h)
@@ -340,8 +350,9 @@ def tile_list_yarn_evenness_page_kernel(
                 for c in range(S // PAGE_CHUNK[0]):
                     interleave_page(0, c, (nc.vector.tensor_copy, nc.scalar.copy)[c])
             if step == SLICES - 1:
-                for c in range(S // PAGE_CHUNK[0]):
-                    quantise_page(0, c)
+                quantise_page(0, 0, EARLY, "factor0")
+            if step == SLICES:
+                quantise_page(0, EARLY, 4 - EARLY, "look1")
 
         def reading_pass(bank, pair, quarter, b):
             for k in range(2):
@@ -360,7 +371,7 @@ def tile_list_yarn_evenness_page_kernel(
                 reading_pass(sums[quarter, pair], pair, quarter, 0)
         for quarter in range(S // QUARTER):
             interleave_page(1, quarter, nc.scalar.copy if quarter == 1 else nc.vector.tensor_copy)
-            quantise_page(1, quarter)
+            quantise_page(1, quarter, 1, "q_codes1_%d" % quarter)
             for pair in range(2):
                 reading_pass(sums[quarter, pair], pair, quarter, 1)
         out_rows = out.rearrange("(c p) j -> p c j", p=PART)

@@ -19,20 +19,19 @@ ACT = mybir.ActivationFunctionType
 PART = 128
 PACK = 4
 PASS = PART * PACK
+QUADS = 4
 GROUPS = H // PASS
 SLICES = GROUPS * PACK
 BANK = 512
+BANKS = 8
 HALVES = S // BANK
 QUARTER = 256
-EARLY = 3
-SKIP_ON_VECTOR = (0, 1, 2, 6,)
-ON_VECTOR = ((2, 1), (3, 1))
-SLOTS = 4
-LAG = 2
-THIRD_TWICE = (2, 3, 7)
-SCALAR_CAST_SHARE = 64
-PAGE_CHUNK = (512, 256)
-SKIP_ON_SCALAR = (3, 4, 5, 7,)
+QUARTERS = S // QUARTER
+ROUND_LAG = 2
+PAGES = 4
+ROUND_WIDTH = (BANK, QUARTER)
+
+THIRD_TWICE = (PACK - 2, PACK - 1, SLICES - 1)
 
 
 def tile_list_yarn_evenness_page_kernel(
@@ -43,40 +42,19 @@ def tile_list_yarn_evenness_page_kernel(
     with ExitStack() as ctx:
         keep = ctx.enter_context(tc.tile_pool(name="keep", bufs=1))
         psum = ctx.enter_context(tc.psum_pool(name="psum", bufs=1))
-        banks = [psum.tile([PART, BANK], F32, name="bank%d" % n) for n in range(8)]
+        banks = [psum.tile([PART, BANK], F32, name="bank%d" % n) for n in range(BANKS)]
 
-        def load_scale_rows(queue, plane, rows):
-            for quad in range(4):
-                queue.dma_start(
+        def load_scale_rows(plane, rows):
+            for quad in range(QUADS):
+                nc.sync.dma_start(
                     out=plane[32 * quad : 32 * quad + 4].bitcast(I32),
                     in_=rows[:, 4 * quad : 4 * quad + 4, :].rearrange("a q c -> q a c").bitcast(I32),
                 )
 
-        offs_sb = keep.tile([PART, S // 16], U16, name="offs_sb")
-        nc.sync.dma_start(offs_sb[:], offs)
-        pos1_sb = keep.tile([PART, P // 16], U16, name="pos1_sb")
-        nc.sync.dma_start(pos1_sb[:], pos1)
-        pos2_sb = keep.tile([PART, P // 16], U16, name="pos2_sb")
-        nc.sync.dma_start(pos2_sb[:], pos2)
-        tab_sb = keep.tile([PART, T], U32, name="tab_sb", align_bytes=64)
-        nc.sync.dma_start(
-            out=tab_sb[:].bitcast(I32), in_=tab_words[0].rearrange("p t i -> p (t i)").bitcast(I32)
-        )
-        w3_raw_plane = keep.tile([PART, 1, H], U8, name="w3_raw_plane", align_bytes=64)
-        nc.gpsimd.memset(w3_raw_plane[:].bitcast(I32), 0)
-        tab_plane = keep.tile([PART, T], U8, name="tab_plane", align_bytes=64)
-        nc.vector.memset(tab_plane[:].bitcast(I32), 0)
-        for quad in range(4):
-            nc.sync.dma_start(
-                out=tab_plane[32 * quad : 32 * quad + 4, :].bitcast(I32),
-                in_=tab_scales[0, 4 * quad : 4 * quad + 4, :].bitcast(I32),
-            )
-
-        def load_rows_vector(vec, name):
-            cols = keep.tile([PART, GROUPS, PACK], F32, name=name)
-            nc.sync.dma_start(out=cols[:], in_=vec.rearrange("(b p t) -> p b t", p=PART, t=PACK))
-            return cols[:].rearrange("p b t -> p (b t)")
-
+        def load_row_values(vec, name):
+            values = keep.tile([PART, GROUPS, PACK], F32, name=name)
+            nc.sync.dma_start(out=values[:], in_=vec.rearrange("(b p t) -> p b t", p=PART, t=PACK))
+            return values[:].rearrange("p b t -> p (b t)")
 
         def load_weight(w, b, name, parts):
             width = PASS // parts
@@ -96,32 +74,50 @@ def tile_list_yarn_evenness_page_kernel(
             )
             return rows
 
-        raw = {}
-        raw[1, 0] = load_weight(w1, 0, "w1_raw0", 2)
-        raw[2, 0] = load_weight(w2, 0, "w2_raw0", 2)
-        w3_raw = keep.tile([PART, 2 * H], U8, name="w3_raw", align_bytes=64)
-        nc.sync.dma_start(out=w3_raw[:].bitcast(I32), in_=w3_words[0].bitcast(I32))
-        load_scale_rows(nc.sync, w3_raw_plane, w3_scales)
-
         def load_wgs(t0):
             rows = keep.tile([PART, 2, P], F32, name="wgs%d" % t0)
-            for quad in range(4):
+            for quad in range(QUADS):
                 nc.sync.dma_start(
                     out=rows[32 * quad : 32 * quad + 32],
                     in_=wgs.rearrange("(p t) m -> p t m", t=PACK)[:, t0 : t0 + 2, :],
                 )
             return [rows[:, 0, :], rows[:, 1, :]]
 
-        slope_sb = load_rows_vector(slope, "slope_sb")
-        thr_sb = load_rows_vector(thr, "thr_sb")
-        skip_sb = load_rows_vector(skip, "skip_sb")
+        offs_sb = keep.tile([PART, S // 16], U16, name="offs_sb")
+        nc.sync.dma_start(offs_sb[:], offs)
+        pos1_sb = keep.tile([PART, P // 16], U16, name="pos1_sb")
+        nc.sync.dma_start(pos1_sb[:], pos1)
+        pos2_sb = keep.tile([PART, P // 16], U16, name="pos2_sb")
+        nc.sync.dma_start(pos2_sb[:], pos2)
+        tab_sb = keep.tile([PART, T], U32, name="tab_sb", align_bytes=64)
+        nc.sync.dma_start(
+            out=tab_sb[:].bitcast(I32), in_=tab_words[0].rearrange("p t i -> p (t i)").bitcast(I32)
+        )
+        w3_raw_plane = keep.tile([PART, 1, H], U8, name="w3_raw_plane", align_bytes=64)
+        nc.gpsimd.memset(w3_raw_plane[:].bitcast(I32), 0)
+        tab_plane = keep.tile([PART, T], U8, name="tab_plane", align_bytes=64)
+        nc.vector.memset(tab_plane[:].bitcast(I32), 0)
+        for quad in range(QUADS):
+            nc.sync.dma_start(
+                out=tab_plane[32 * quad : 32 * quad + 4, :].bitcast(I32),
+                in_=tab_scales[0, 4 * quad : 4 * quad + 4, :].bitcast(I32),
+            )
+        raw = {}
+        raw[1, 0] = load_weight(w1, 0, "w1_raw0", 2)
+        raw[2, 0] = load_weight(w2, 0, "w2_raw0", 2)
+        w3_raw = keep.tile([PART, 2 * H], U8, name="w3_raw", align_bytes=64)
+        nc.sync.dma_start(out=w3_raw[:].bitcast(I32), in_=w3_words[0].bitcast(I32))
+        load_scale_rows(w3_raw_plane, w3_scales)
+        slope_sb = load_row_values(slope, "slope_sb")
+        thr_sb = load_row_values(thr, "thr_sb")
+        skip_sb = load_row_values(skip, "skip_sb")
         wgs_sb = load_wgs(0)
         pat_sb = [load_pat(0), load_pat(1)]
         raw[1, 1] = load_weight(w1, 1, "w1_raw1", 1)
         raw[2, 1] = load_weight(w2, 1, "w2_raw1", 1)
         wgs_sb.extend(load_wgs(2))
         pat_sb.append(load_pat(2))
-        gain_sb = load_rows_vector(gain, "gain_sb")
+        gain_sb = load_row_values(gain, "gain_sb")
         pat_sb.extend(load_pat(s) for s in range(3, SLICES))
         w4_sb = keep.tile([PART, GROUPS, N], U32, name="w4_sb", align_bytes=64)
         nc.sync.dma_start(
@@ -129,30 +125,28 @@ def tile_list_yarn_evenness_page_kernel(
         )
         w4_plane = keep.tile([PART, GROUPS, N], U8, name="w4_plane", align_bytes=64)
         nc.gpsimd.memset(w4_plane[:].bitcast(I32), 0)
-        load_scale_rows(nc.sync, w4_plane, w4_scales)
+        load_scale_rows(w4_plane, w4_scales)
         beta_sb = keep.tile([PART, N // PART], F32, name="beta_sb")
         with nc.allow_non_contiguous_dma(reason="one bias value a partition"):
             nc.sync.dma_start(out=beta_sb[:], in_=beta.rearrange("(c p) -> p c", p=PART))
 
-        w3_codes = keep.tile([PART, 2 * H], U8, name="w3_codes", align_bytes=64)
-
+        picks = [offs_sb[:, half * BANK // 16 : (half + 1) * BANK // 16] for half in range(HALVES)]
         v_codes, v_plane = [], []
         for half in range(HALVES):
-            picks = offs_sb[:, half * BANK // 16 : (half + 1) * BANK // 16]
-            words = keep.tile([PART, BANK], U32, name="v_codes%d" % half, align_bytes=64)
-            nc.vector.tensor_copy(out=words[:], in_=tab_sb[:].indirect(picks))
-            plane = keep.tile([PART, BANK], U8, name="v_plane%d" % half, align_bytes=64)
-            nc.vector.tensor_copy(out=plane[:], in_=tab_plane[:].indirect(picks))
-            v_codes.append(words)
-            v_plane.append(plane)
+            v_codes.append(keep.tile([PART, BANK], U32, name="v_codes%d" % half, align_bytes=64))
+            nc.vector.tensor_copy(out=v_codes[half][:], in_=tab_sb[:].indirect(picks[half]))
+        for half in range(HALVES):
+            v_plane.append(keep.tile([PART, BANK], U8, name="v_plane%d" % half, align_bytes=64))
+            nc.vector.tensor_copy(out=v_plane[half][:], in_=tab_plane[:].indirect(picks[half]))
 
         w_codes, w_plane = {}, {}
 
-        def round_weight(key, shares, tag):
+        def round_weight(key, copies, tag):
             grouped = keep.tile([PART, PACK, PART, PACK], BF16, name="w%d_grouped%d" % key, tag=tag, align_bytes=64)
             dealt = grouped[:].rearrange("p t m j -> p m j t")
             span = PART // len(raw[key])
-            for copy, m0, m1 in shares:
+            for n, copy in enumerate(copies):
+                m0, m1 = n * PART // 2, (n + 1) * PART // 2
                 source = raw[key][m0 // span][:].rearrange("p j (m t) -> p m j t", t=PACK)
                 copy(out=dealt[:, m0:m1], in_=source[:, m0 % span : m0 % span + m1 - m0])
             return grouped
@@ -168,20 +162,23 @@ def tile_list_yarn_evenness_page_kernel(
                     in_=flat[:, t0 * PASS : t1 * PASS],
                 )
 
-        on_scalar = [(nc.scalar.copy, 0, PART // 2), (nc.scalar.copy, PART // 2, PART)]
-        quantise_weight((1, 0), round_weight((1, 0), on_scalar, "w1_grouped0"), [(0, PACK)], "w1_codes0")
-        shared = [(nc.scalar.copy, 0, SCALAR_CAST_SHARE), (nc.vector.tensor_copy, SCALAR_CAST_SHARE, PART)]
-        quantise_weight((2, 0), round_weight((2, 0), shared, "w2_grouped0"), [(0, 1), (1, PACK)], "w2_codes0")
+        on_scalar = (nc.scalar.copy, nc.scalar.copy)
+        whole = [(0, PACK)]
+        quantise_weight((1, 0), round_weight((1, 0), on_scalar, "w1_grouped0"), whole, "w1_codes0")
+        grouped_w2 = round_weight((2, 0), (nc.scalar.copy, nc.vector.tensor_copy), "w2_grouped0")
+        quantise_weight((2, 0), grouped_w2, [(0, 1), (1, PACK)], "w2_codes0")
 
+        w3_codes = keep.tile([PART, 2 * H], U8, name="w3_codes", align_bytes=64)
         w3_plane = keep.tile([PART, H], U8, name="w3_plane", align_bytes=64)
         for b in range(GROUPS):
+            group = slice(PASS * b, PASS * (b + 1))
             nc.vector.tensor_copy(
-                out=w3_codes[:].bitcast(U16)[:, PASS * b : PASS * (b + 1)].rearrange("p (t m) -> p t m", t=PACK),
-                in_=w3_raw[:].bitcast(U16)[:, PASS * b : PASS * (b + 1)].rearrange("p (m t) -> p t m", t=PACK),
+                out=w3_codes[:].bitcast(U16)[:, group].rearrange("p (t m) -> p t m", t=PACK),
+                in_=w3_raw[:].bitcast(U16)[:, group].rearrange("p (m t) -> p t m", t=PACK),
             )
             nc.vector.tensor_copy(
-                out=w3_plane[:, PASS * b : PASS * (b + 1)].rearrange("p (t m) -> p t m", t=PACK),
-                in_=w3_raw_plane[:, 0, PASS * b : PASS * (b + 1)].rearrange("p (m t) -> p t m", t=PACK),
+                out=w3_plane[:, group].rearrange("p (t m) -> p t m", t=PACK),
+                in_=w3_raw_plane[:, 0, group].rearrange("p (m t) -> p t m", t=PACK),
             )
 
         def stationary(which, s):
@@ -191,23 +188,20 @@ def tile_list_yarn_evenness_page_kernel(
                     w3_codes[:, 2 * PART * s : 2 * PART * (s + 1)].bitcast(FP4X4),
                     w3_plane[:, PART * s : PART * (s + 1)],
                 )
-            cols = slice(PART * t, PART * (t + 1))
-            return w_codes[which, b][:, cols].bitcast(FP8X4), w_plane[which, b][:, cols]
+            places = slice(PART * t, PART * (t + 1))
+            return w_codes[which, b][:, places].bitcast(FP8X4), w_plane[which, b][:, places]
 
         def ring(name, count, width):
             return [keep.tile([PART, width], F32, name="%s%d" % (name, n), align_bytes=64) for n in range(count)]
 
         thin_ring, h_ring = ring("thin", 2, S), ring("h", 2, S)
-        look_ring, factor_ring, page_ring = ring("look", 2, P), ring("factor", 2, P), ring("page", SLOTS, S)
+        look_ring, factor_ring, page_ring = ring("look", 2, P), ring("factor", 2, P), ring("page", PAGES, S)
         early_look = ring("early_look", 2, P)
-
-        def thin_tile(s):
-            return thin_ring[min(s, 1)]
 
         taken = []
 
         def take_bank():
-            taken.append(banks[len(taken) % len(banks)])
+            taken.append(banks[len(taken) % BANKS])
             return taken[-1]
 
         def product(s, half, weights):
@@ -221,173 +215,170 @@ def tile_list_yarn_evenness_page_kernel(
                 )
             return bank
 
-        cols = [slice(half * BANK, (half + 1) * BANK) for half in range(HALVES)]
+        half_cols = [slice(half * BANK, (half + 1) * BANK) for half in range(HALVES)]
 
         def first_response(s):
             for half in range(HALVES):
                 bank = product(s, half, (1, 3) if s in THIRD_TWICE else (1,))
-                nc.scalar.copy(out=thin_tile(s)[:, cols[half]], in_=bank[:])
+                nc.scalar.copy(out=thin_ring[min(s, 1)][:, half_cols[half]], in_=bank[:])
 
         def features(s):
-            twice = s in THIRD_TWICE
-            thin = thin_tile(s)
-            h = h_ring[s % 2]
+            thin, h = thin_ring[min(s, 1)], h_ring[s % 2]
             for half in range(HALVES):
-                bank = product(s, half, (2, 3) if twice else (2,))
+                bank = product(s, half, (2, 3) if s in THIRD_TWICE else (2,))
                 nc.vector.tensor_tensor(
-                    out=h[:, cols[half]], in0=bank[:], in1=thin[:, cols[half]], op=ALU.max
+                    out=h[:, half_cols[half]], in0=bank[:], in1=thin[:, half_cols[half]], op=ALU.max
                 )
-            if not twice:
+            if s not in THIRD_TWICE:
                 for half in range(HALVES):
                     bank = product(s, half, (3,))
                     nc.vector.tensor_tensor(
-                        out=h[:, cols[half]], in0=bank[:], in1=h[:, cols[half]], op=ALU.add
+                        out=h[:, half_cols[half]], in0=bank[:], in1=h[:, half_cols[half]], op=ALU.add
                     )
-            return h
 
-        def fill_page(s):
-            h = h_ring[s % 2]
-            page = page_ring[s % SLOTS]
-            if s in SKIP_ON_SCALAR:
-                nc.scalar.activation(out=page[:], in_=h[:], func=ACT.Copy, scale=skip_sb[:, s : s + 1])
-            elif s in SKIP_ON_VECTOR:
-                nc.vector.tensor_scalar(
-                    out=page[:], in0=h[:], scalar1=skip_sb[:, s : s + 1], scalar2=None, op0=ALU.mult
-                )
-            else:
-                nc.gpsimd.tensor_scalar(
-                    out=page[:], in0=h[:], scalar1=skip_sb[:, s : s + 1], scalar2=0.0,
-                    op0=ALU.mult, op1=ALU.add,
-                )
+        def look_tile(s):
+            return early_look[s] if s < 2 else look_ring[s % 2]
 
-        def look_and_page(s, h):
-            look = early_look[s] if s < 2 else look_ring[s % 2]
+        def take_look(s):
             nc.scalar.activation(
-                out=look[:], in_=h[:].indirect(pos1_sb[:]), func=ACT.Sigmoid,
+                out=look_tile(s)[:], in_=h_ring[s % 2][:].indirect(pos1_sb[:]), func=ACT.Sigmoid,
                 bias=thr_sb[:, s : s + 1], scale=slope_sb[:, s : s + 1],
             )
-            page = page_ring[s % SLOTS]
-            if s > 0:
-                fill_page(s)
-            factor = factor_ring[s % 2]
+
+        def fill_page(s):
+            h, page, skip_s = h_ring[s % 2], page_ring[s % PAGES], skip_sb[:, s : s + 1]
+            if s < PACK - 1:
+                nc.vector.tensor_scalar(out=page[:], in0=h[:], scalar1=skip_s, scalar2=None, op0=ALU.mult)
+            elif s >= PACK and s + 1 < SLICES and s + 1 not in THIRD_TWICE:
+                nc.gpsimd.tensor_scalar(
+                    out=page[:], in0=h[:], scalar1=skip_s, scalar2=0.0, op0=ALU.mult, op1=ALU.add
+                )
+            else:
+                nc.scalar.activation(out=page[:], in_=h[:], func=ACT.Copy, scale=skip_s)
+
+        def make_factor(s):
             nc.gpsimd.tensor_tensor(
-                out=factor[:], in0=pat_sb[s][:], in1=wgs_sb[s % PACK], op=ALU.mult
+                out=factor_ring[s % 2][:], in0=pat_sb[s][:], in1=wgs_sb[s % PACK], op=ALU.mult
             )
-            return look, factor, page
 
-        def write_page(look, factor, page):
-            nc.vector.tensor_tensor(out=page[:].indirect(pos2_sb[:]), in0=look[:], in1=factor[:], op=ALU.mult)
+        def write_page(s):
+            nc.vector.tensor_tensor(
+                out=page_ring[s % PAGES][:].indirect(pos2_sb[:]),
+                in0=look_tile(s)[:], in1=factor_ring[s % 2][:], op=ALU.mult,
+            )
 
-        rounded = {}
+        rounded, q_grouped, q_codes, q_plane = {}, {}, {}, {}
 
-        def round_page(s, page):
+        def round_page(s):
             b, t = divmod(s, PACK)
-            width = PAGE_CHUNK[b]
+            width = ROUND_WIDTH[b]
             for c in range(S // width):
                 if t == 0:
-                    rounded[b, c] = keep.tile([PART, PACK, width], BF16, name="rounded%d_%d" % (b, c))
+                    rounded[b, c] = keep.tile([PART, PACK * width], BF16, name="rounded%d_%d" % (b, c))
+                if b == 0:
+                    target = rounded[b, c][:, t * width : (t + 1) * width]
+                else:
+                    target = rounded[b, c][:].rearrange("p (u j e) -> p u j e", u=2, e=2)[:, t // 2, :, t % 2]
                 nc.scalar.activation(
-                    out=rounded[b, c][:, t, :], in_=page[:, c * width : (c + 1) * width],
+                    out=target, in_=page_ring[s % PAGES][:, c * width : (c + 1) * width],
                     func=ACT.Copy, scale=gain_sb[:, s : s + 1],
                 )
 
-        q_codes, q_plane = {}, {}
-
-        q_grouped = {}
-
-        def interleave_page(b, c, copy):
-            width = PAGE_CHUNK[b]
-            name = "q_grouped%d_%d" % (b, c)
-            if b == 0:
-                grouped = keep.tile([PART, PACK * width], BF16, name=name, tag=("pat6", "pat5")[c], align_bytes=64)[:]
-            elif c < 2:
-                grouped = keep.tile([PART, PACK * width], BF16, name=name, align_bytes=64)[:]
-            else:
-                if c == 2:
-                    q_grouped["rest"] = keep.tile([PART, 2 * PACK * width], BF16, name=name, tag="q_grouped1_0", align_bytes=64)
-                grouped = q_grouped["rest"][:, (c - 2) * PACK * width : (c - 1) * PACK * width]
-            copy(
-                out=grouped.rearrange("p (j i t) -> p j t i", i=PACK, t=PACK),
-                in_=rounded[b, c][:].rearrange("p t (j i) -> p j t i", i=PACK),
+        def interleave_slices(c, copy, tag):
+            q_grouped[0, c] = keep.tile(
+                [PART, PACK * ROUND_WIDTH[0]], BF16, name="q_grouped0_%d" % c, tag=tag, align_bytes=64
             )
-            q_grouped[b, c] = grouped
+            copy(
+                out=q_grouped[0, c][:].rearrange("p (j i t) -> p j t i", i=PACK, t=PACK),
+                in_=rounded[0, c][:].rearrange("p (t j i) -> p j t i", t=PACK, i=PACK),
+            )
 
-        def quantise_page(b, first, count, tag):
-            name = "q%d_%d" % (b, first)
-            codes = keep.tile([PART, count * QUARTER], U32, name=name + "_codes", tag=tag, align_bytes=64)
-            plane = keep.tile([PART, count * QUARTER], U8, name=name + "_plane", align_bytes=64)
-            for k in range(count):
-                c, col = divmod((first + k) * QUARTER, PAGE_CHUNK[b])
-                cols_k = slice(k * QUARTER, (k + 1) * QUARTER)
-                q_codes[b, first + k], q_plane[b, first + k] = codes[:, cols_k], plane[:, cols_k]
+        def interleave_pairs(c):
+            q_grouped[1, c] = keep.tile(
+                [PART, PACK * ROUND_WIDTH[1]], BF16, name="q_grouped1_%d" % c, align_bytes=64
+            )
+            nc.vector.tensor_copy(
+                out=q_grouped[1, c][:].bitcast(F32).rearrange("p (j u) -> p j u", u=2),
+                in_=rounded[1, c][:].bitcast(F32).rearrange("p (u j) -> p j u", u=2),
+            )
+
+        def quantise_page(b, quarters, tag):
+            name = "q%d_%d" % (b, quarters.start)
+            codes = keep.tile([PART, len(quarters) * QUARTER], U32, name=name + "_codes", tag=tag, align_bytes=64)
+            plane = keep.tile([PART, len(quarters) * QUARTER], U8, name=name + "_plane", align_bytes=64)
+            for n, quarter in enumerate(quarters):
+                c, j0 = divmod(quarter * QUARTER, ROUND_WIDTH[b])
+                q_codes[b, quarter] = codes[:, n * QUARTER : (n + 1) * QUARTER]
+                q_plane[b, quarter] = plane[:, n * QUARTER : (n + 1) * QUARTER]
                 nc.vector.quantize_mx(
-                    out=codes[:, cols_k].bitcast(FP8X4), scales=plane[:, cols_k],
-                    in_=q_grouped[b, c][:, PACK * col : PACK * (col + QUARTER)],
+                    out=q_codes[b, quarter].bitcast(FP8X4), scales=q_plane[b, quarter],
+                    in_=q_grouped[b, c][:, PACK * j0 : PACK * (j0 + QUARTER)],
                 )
 
-        made = {}
         first_response(0)
-        for step in range(SLICES + LAG):
+        for step in range(SLICES + ROUND_LAG):
             if step < SLICES:
-                h = features(step)
-            if step == 1:
-                fill_page(step - 1)
-            if step < SLICES:
+                features(step)
+                if step == 1:
+                    fill_page(0)
                 if step + 1 < SLICES:
                     first_response(step + 1)
-                made[step] = look_and_page(step, h)
+                take_look(step)
+                if step > 0:
+                    fill_page(step)
+                make_factor(step)
             if 1 <= step <= SLICES:
-                write_page(*made[step - 1])
-            if step >= LAG:
-                round_page(step - LAG, made[step - LAG][2])
+                write_page(step - 1)
+            if step >= ROUND_LAG:
+                round_page(step - ROUND_LAG)
             if step == 1:
-                late1 = round_weight((1, 1), on_scalar, "pat1")
-                late2 = round_weight((2, 1), on_scalar, "early_look0")
+                late_w1 = round_weight((1, 1), on_scalar, "pat1")
+                late_w2 = round_weight((2, 1), on_scalar, "early_look0")
             if step == 2:
-                quantise_weight((1, 1), late1, [(0, PACK)], "pat2")
-                quantise_weight((2, 1), late2, [(0, PACK)], "early_look1")
-            if step == PACK - 1 + LAG:
-                for c in range(S // PAGE_CHUNK[0]):
-                    interleave_page(0, c, (nc.vector.tensor_copy, nc.scalar.copy)[c])
+                quantise_weight((1, 1), late_w1, whole, "pat2")
+                quantise_weight((2, 1), late_w2, whole, "early_look1")
+            if step == PACK - 1 + ROUND_LAG:
+                interleave_slices(0, nc.vector.tensor_copy, "pat6")
+                interleave_slices(1, nc.scalar.copy, "pat5")
             if step == SLICES - 1:
-                quantise_page(0, 0, EARLY, "factor0")
+                quantise_page(0, range(0, QUARTERS - 1), "factor0")
             if step == SLICES:
-                quantise_page(0, EARLY, 4 - EARLY, "look1")
+                quantise_page(0, range(QUARTERS - 1, QUARTERS), "look1")
 
-        def reading_pass(bank, pair, quarter, b):
-            for k in range(2):
-                rows = slice((2 * pair + k) * PART, (2 * pair + k + 1) * PART)
+        def reading_passes(bank, side, quarter, b):
+            for n in range(2):
+                rows = slice((2 * side + n) * PART, (2 * side + n + 1) * PART)
                 nc.tensor.matmul_mx(
-                    out=bank[:, k * QUARTER : (k + 1) * QUARTER],
+                    out=bank[:, n * QUARTER : (n + 1) * QUARTER],
                     lhsT=w4_sb[:, b, rows].bitcast(FP8X4), lhsT_scale=w4_plane[:, b, rows],
                     rhs=q_codes[b, quarter].bitcast(FP8X4), rhs_scale=q_plane[b, quarter],
-                    start=(b == 0 and k == 0), stop=(b == GROUPS - 1 and k == 1),
+                    start=(b == 0 and n == 0), stop=(b == GROUPS - 1 and n == 1),
                 )
 
         sums = {}
-        for quarter in range(S // QUARTER):
-            for pair in range(2):
-                sums[quarter, pair] = take_bank()
-                reading_pass(sums[quarter, pair], pair, quarter, 0)
-        for quarter in range(S // QUARTER):
-            interleave_page(1, quarter, nc.scalar.copy if quarter == 1 else nc.vector.tensor_copy)
-            quantise_page(1, quarter, 1, "q_codes1_%d" % quarter)
-            for pair in range(2):
-                reading_pass(sums[quarter, pair], pair, quarter, 1)
+        for quarter in range(QUARTERS):
+            for side in range(2):
+                sums[quarter, side] = take_bank()
+                reading_passes(sums[quarter, side], side, quarter, 0)
+        for quarter in range(QUARTERS):
+            interleave_pairs(quarter)
+            quantise_page(1, range(quarter, quarter + 1), "q_codes1_%d" % quarter)
+            for side in range(2):
+                reading_passes(sums[quarter, side], side, quarter, 1)
         out_rows = out.rearrange("(c p) j -> p c j", p=PART)
-        for quarter in range(S // QUARTER):
-            for pair in range(2):
-                scores = keep.tile([PART, 2, QUARTER], F32, name="scores%d_%d" % (quarter, pair))
-                for k in range(2):
-                    bias = beta_sb[:, 2 * pair + k : 2 * pair + k + 1]
-                    part = sums[quarter, pair][:, k * QUARTER : (k + 1) * QUARTER]
-                    if (quarter, pair) in ON_VECTOR:
+        for quarter in range(QUARTERS):
+            for side in range(2):
+                scores = keep.tile([PART, 2, QUARTER], F32, name="scores%d_%d" % (quarter, side))
+                for n in range(2):
+                    bias = beta_sb[:, 2 * side + n : 2 * side + n + 1]
+                    tile_sums = sums[quarter, side][:, n * QUARTER : (n + 1) * QUARTER]
+                    if side == 1 and quarter >= QUARTERS // 2:
                         nc.vector.tensor_scalar(
-                            out=scores[:, k, :], in0=part, scalar1=bias, scalar2=None, op0=ALU.add
+                            out=scores[:, n, :], in0=tile_sums, scalar1=bias, scalar2=None, op0=ALU.add
                         )
                     else:
-                        nc.scalar.activation(out=scores[:, k, :], in_=part, func=ACT.Identity, bias=bias)
+                        nc.scalar.activation(out=scores[:, n, :], in_=tile_sums, func=ACT.Identity, bias=bias)
                 nc.sync.dma_start(
-                    out=out_rows[:, 2 * pair : 2 * pair + 2, quarter * QUARTER : (quarter + 1) * QUARTER],
+                    out=out_rows[:, 2 * side : 2 * side + 2, quarter * QUARTER : (quarter + 1) * QUARTER],
                     in_=scores[:],
                 )

from contextlib import ExitStack

import concourse.mybir as mybir

K, H, N, T, S, P = 512, 1024, 512, 2048, 1024, 512
FLOPS = 2 * K * H * S * 3 + 2 * H * N * S

F32 = mybir.dt.float32
BF16 = mybir.dt.bfloat16
I32 = mybir.dt.int32
U32 = mybir.dt.uint32
U16 = mybir.dt.uint16
U8 = mybir.dt.uint8
FP8X4 = mybir.dt.float8_e4m3fn_x4
FP4X4 = mybir.dt.float4_e2m1fn_x4
ALU = mybir.AluOpType
ACT = mybir.ActivationFunctionType

PART = 128
PACK = 4
PASS = PART * PACK
QUADS = 4
GROUPS = H // PASS
SLICES = GROUPS * PACK
BANK = 512
BANKS = 8
HALVES = S // BANK
QUARTER = 256
QUARTERS = S // QUARTER
ROUND_LAG = 2
PAGES = 4
ROUND_WIDTH = (BANK, QUARTER)

THIRD_TWICE = (PACK - 2, PACK - 1, SLICES - 1)


def tile_list_yarn_evenness_page_kernel(
    tc, tab_words, tab_scales, offs, pos1, pos2, w1, w2, w3_words, w3_scales,
    slope, thr, pat, skip, wgs, gain, w4_words, w4_scales, beta, out,
):
    nc = tc.nc
    with ExitStack() as ctx:
        keep = ctx.enter_context(tc.tile_pool(name="keep", bufs=1))
        psum = ctx.enter_context(tc.psum_pool(name="psum", bufs=1))
        banks = [psum.tile([PART, BANK], F32, name="bank%d" % n) for n in range(BANKS)]

        def load_scale_rows(plane, rows):
            for quad in range(QUADS):
                nc.sync.dma_start(
                    out=plane[32 * quad : 32 * quad + 4].bitcast(I32),
                    in_=rows[:, 4 * quad : 4 * quad + 4, :].rearrange("a q c -> q a c").bitcast(I32),
                )

        def load_row_values(vec, name):
            values = keep.tile([PART, GROUPS, PACK], F32, name=name)
            nc.sync.dma_start(out=values[:], in_=vec.rearrange("(b p t) -> p b t", p=PART, t=PACK))
            return values[:].rearrange("p b t -> p (b t)")

        def load_weight(w, b, name, parts):
            width = PASS // parts
            tiles = []
            for n in range(parts):
                part = keep.tile([PART, PACK, width], F32, name="%s_%d" % (name, n))
                c0 = b * PASS + n * width
                nc.sync.dma_start(out=part[:], in_=w.rearrange("(p j) c -> p j c", j=PACK)[:, :, c0 : c0 + width])
                tiles.append(part)
            return tiles

        def load_pat(s):
            b, t = divmod(s, PACK)
            rows = keep.tile([PART, P], F32, name="pat%d" % s, align_bytes=64)
            nc.sync.dma_start(
                out=rows[:], in_=pat.rearrange("(b p t) m -> p b t m", p=PART, t=PACK)[:, b, t, :]
            )
            return rows

        def load_wgs(t0):
            rows = keep.tile([PART, 2, P], F32, name="wgs%d" % t0)
            for quad in range(QUADS):
                nc.sync.dma_start(
                    out=rows[32 * quad : 32 * quad + 32],
                    in_=wgs.rearrange("(p t) m -> p t m", t=PACK)[:, t0 : t0 + 2, :],
                )
            return [rows[:, 0, :], rows[:, 1, :]]

        offs_sb = keep.tile([PART, S // 16], U16, name="offs_sb")
        nc.sync.dma_start(offs_sb[:], offs)
        pos1_sb = keep.tile([PART, P // 16], U16, name="pos1_sb")
        nc.sync.dma_start(pos1_sb[:], pos1)
        pos2_sb = keep.tile([PART, P // 16], U16, name="pos2_sb")
        nc.sync.dma_start(pos2_sb[:], pos2)
        tab_sb = keep.tile([PART, T], U32, name="tab_sb", align_bytes=64)
        nc.sync.dma_start(
            out=tab_sb[:].bitcast(I32), in_=tab_words[0].rearrange("p t i -> p (t i)").bitcast(I32)
        )
        w3_raw_plane = keep.tile([PART, 1, H], U8, name="w3_raw_plane", align_bytes=64)
        nc.gpsimd.memset(w3_raw_plane[:].bitcast(I32), 0)
        tab_plane = keep.tile([PART, T], U8, name="tab_plane", align_bytes=64)
        nc.vector.memset(tab_plane[:].bitcast(I32), 0)
        for quad in range(QUADS):
            nc.sync.dma_start(
                out=tab_plane[32 * quad : 32 * quad + 4, :].bitcast(I32),
                in_=tab_scales[0, 4 * quad : 4 * quad + 4, :].bitcast(I32),
            )
        raw = {}
        raw[1, 0] = load_weight(w1, 0, "w1_raw0", 2)
        raw[2, 0] = load_weight(w2, 0, "w2_raw0", 2)
        w3_raw = keep.tile([PART, 2 * H], U8, name="w3_raw", align_bytes=64)
        nc.sync.dma_start(out=w3_raw[:].bitcast(I32), in_=w3_words[0].bitcast(I32))
        load_scale_rows(w3_raw_plane, w3_scales)
        slope_sb = load_row_values(slope, "slope_sb")
        thr_sb = load_row_values(thr, "thr_sb")
        skip_sb = load_row_values(skip, "skip_sb")
        wgs_sb = load_wgs(0)
        pat_sb = [load_pat(0), load_pat(1)]
        raw[1, 1] = load_weight(w1, 1, "w1_raw1", 1)
        raw[2, 1] = load_weight(w2, 1, "w2_raw1", 1)
        wgs_sb.extend(load_wgs(2))
        pat_sb.append(load_pat(2))
        gain_sb = load_row_values(gain, "gain_sb")
        pat_sb.extend(load_pat(s) for s in range(3, SLICES))
        w4_sb = keep.tile([PART, GROUPS, N], U32, name="w4_sb", align_bytes=64)
        nc.sync.dma_start(
            out=w4_sb[:].bitcast(I32), in_=w4_words.rearrange("a p c i -> p a (c i)").bitcast(I32)
        )
        w4_plane = keep.tile([PART, GROUPS, N], U8, name="w4_plane", align_bytes=64)
        nc.gpsimd.memset(w4_plane[:].bitcast(I32), 0)
        load_scale_rows(w4_plane, w4_scales)
        beta_sb = keep.tile([PART, N // PART], F32, name="beta_sb")
        with nc.allow_non_contiguous_dma(reason="one bias value a partition"):
            nc.sync.dma_start(out=beta_sb[:], in_=beta.rearrange("(c p) -> p c", p=PART))

        picks = [offs_sb[:, half * BANK // 16 : (half + 1) * BANK // 16] for half in range(HALVES)]
        v_codes, v_plane = [], []
        for half in range(HALVES):
            v_codes.append(keep.tile([PART, BANK], U32, name="v_codes%d" % half, align_bytes=64))
            nc.vector.tensor_copy(out=v_codes[half][:], in_=tab_sb[:].indirect(picks[half]))
        for half in range(HALVES):
            v_plane.append(keep.tile([PART, BANK], U8, name="v_plane%d" % half, align_bytes=64))
            nc.vector.tensor_copy(out=v_plane[half][:], in_=tab_plane[:].indirect(picks[half]))

        w_codes, w_plane = {}, {}

        def round_weight(key, copies, tag):
            grouped = keep.tile([PART, PACK, PART, PACK], BF16, name="w%d_grouped%d" % key, tag=tag, align_bytes=64)
            dealt = grouped[:].rearrange("p t m j -> p m j t")
            span = PART // len(raw[key])
            for n, copy in enumerate(copies):
                m0, m1 = n * PART // 2, (n + 1) * PART // 2
                source = raw[key][m0 // span][:].rearrange("p j (m t) -> p m j t", t=PACK)
                copy(out=dealt[:, m0:m1], in_=source[:, m0 % span : m0 % span + m1 - m0])
            return grouped

        def quantise_weight(key, grouped, cuts, tag):
            w_codes[key] = keep.tile([PART, PASS], U32, name="w%d_codes%d" % key, tag=tag, align_bytes=64)
            w_plane[key] = keep.tile([PART, PASS], U8, name="w%d_plane%d" % key, align_bytes=64)
            flat = grouped[:].rearrange("p t m j -> p (t m j)")
            for t0, t1 in cuts:
                nc.vector.quantize_mx(
                    out=w_codes[key][:, t0 * PART : t1 * PART].bitcast(FP8X4),
                    scales=w_plane[key][:, t0 * PART : t1 * PART],
                    in_=flat[:, t0 * PASS : t1 * PASS],
                )

        on_scalar = (nc.scalar.copy, nc.scalar.copy)
        whole = [(0, PACK)]
        quantise_weight((1, 0), round_weight((1, 0), on_scalar, "w1_grouped0"), whole, "w1_codes0")
        grouped_w2 = round_weight((2, 0), (nc.scalar.copy, nc.vector.tensor_copy), "w2_grouped0")
        quantise_weight((2, 0), grouped_w2, [(0, 1), (1, PACK)], "w2_codes0")

        w3_codes = keep.tile([PART, 2 * H], U8, name="w3_codes", align_bytes=64)
        w3_plane = keep.tile([PART, H], U8, name="w3_plane", align_bytes=64)
        for b in range(GROUPS):
            group = slice(PASS * b, PASS * (b + 1))
            nc.vector.tensor_copy(
                out=w3_codes[:].bitcast(U16)[:, group].rearrange("p (t m) -> p t m", t=PACK),
                in_=w3_raw[:].bitcast(U16)[:, group].rearrange("p (m t) -> p t m", t=PACK),
            )
            nc.vector.tensor_copy(
                out=w3_plane[:, group].rearrange("p (t m) -> p t m", t=PACK),
                in_=w3_raw_plane[:, 0, group].rearrange("p (m t) -> p t m", t=PACK),
            )

        def stationary(which, s):
            b, t = divmod(s, PACK)
            if which == 3:
                return (
                    w3_codes[:, 2 * PART * s : 2 * PART * (s + 1)].bitcast(FP4X4),
                    w3_plane[:, PART * s : PART * (s + 1)],
                )
            places = slice(PART * t, PART * (t + 1))
            return w_codes[which, b][:, places].bitcast(FP8X4), w_plane[which, b][:, places]

        def ring(name, count, width):
            return [keep.tile([PART, width], F32, name="%s%d" % (name, n), align_bytes=64) for n in range(count)]

        thin_ring, h_ring = ring("thin", 2, S), ring("h", 2, S)
        look_ring, factor_ring, page_ring = ring("look", 2, P), ring("factor", 2, P), ring("page", PAGES, S)
        early_look = ring("early_look", 2, P)

        taken = []

        def take_bank():
            taken.append(banks[len(taken) % BANKS])
            return taken[-1]

        def product(s, half, weights):
            bank = take_bank()
            for n, which in enumerate(weights):
                codes, plane = stationary(which, s)
                nc.tensor.matmul_mx(
                    out=bank[:], lhsT=codes, lhsT_scale=plane,
                    rhs=v_codes[half][:].bitcast(FP8X4), rhs_scale=v_plane[half][:],
                    start=(n == 0), stop=(n == len(weights) - 1),
                )
            return bank

        half_cols = [slice(half * BANK, (half + 1) * BANK) for half in range(HALVES)]

        def first_response(s):
            for half in range(HALVES):
                bank = product(s, half, (1, 3) if s in THIRD_TWICE else (1,))
                nc.scalar.copy(out=thin_ring[min(s, 1)][:, half_cols[half]], in_=bank[:])

        def features(s):
            thin, h = thin_ring[min(s, 1)], h_ring[s % 2]
            for half in range(HALVES):
                bank = product(s, half, (2, 3) if s in THIRD_TWICE else (2,))
                nc.vector.tensor_tensor(
                    out=h[:, half_cols[half]], in0=bank[:], in1=thin[:, half_cols[half]], op=ALU.max
                )
            if s not in THIRD_TWICE:
                for half in range(HALVES):
                    bank = product(s, half, (3,))
                    nc.vector.tensor_tensor(
                        out=h[:, half_cols[half]], in0=bank[:], in1=h[:, half_cols[half]], op=ALU.add
                    )

        def look_tile(s):
            return early_look[s] if s < 2 else look_ring[s % 2]

        def take_look(s):
            nc.scalar.activation(
                out=look_tile(s)[:], in_=h_ring[s % 2][:].indirect(pos1_sb[:]), func=ACT.Sigmoid,
                bias=thr_sb[:, s : s + 1], scale=slope_sb[:, s : s + 1],
            )

        def fill_page(s):
            h, page, skip_s = h_ring[s % 2], page_ring[s % PAGES], skip_sb[:, s : s + 1]
            if s < PACK - 1:
                nc.vector.tensor_scalar(out=page[:], in0=h[:], scalar1=skip_s, scalar2=None, op0=ALU.mult)
            elif s >= PACK and s + 1 < SLICES and s + 1 not in THIRD_TWICE:
                nc.gpsimd.tensor_scalar(
                    out=page[:], in0=h[:], scalar1=skip_s, scalar2=0.0, op0=ALU.mult, op1=ALU.add
                )
            else:
                nc.scalar.activation(out=page[:], in_=h[:], func=ACT.Copy, scale=skip_s)

        def make_factor(s):
            nc.gpsimd.tensor_tensor(
                out=factor_ring[s % 2][:], in0=pat_sb[s][:], in1=wgs_sb[s % PACK], op=ALU.mult
            )

        def write_page(s):
            nc.vector.tensor_tensor(
                out=page_ring[s % PAGES][:].indirect(pos2_sb[:]),
                in0=look_tile(s)[:], in1=factor_ring[s % 2][:], op=ALU.mult,
            )

        rounded, q_grouped, q_codes, q_plane = {}, {}, {}, {}

        def round_page(s):
            b, t = divmod(s, PACK)
            width = ROUND_WIDTH[b]
            for c in range(S // width):
                if t == 0:
                    rounded[b, c] = keep.tile([PART, PACK * width], BF16, name="rounded%d_%d" % (b, c))
                if b == 0:
                    target = rounded[b, c][:, t * width : (t + 1) * width]
                else:
                    target = rounded[b, c][:].rearrange("p (u j e) -> p u j e", u=2, e=2)[:, t // 2, :, t % 2]
                nc.scalar.activation(
                    out=target, in_=page_ring[s % PAGES][:, c * width : (c + 1) * width],
                    func=ACT.Copy, scale=gain_sb[:, s : s + 1],
                )

        def interleave_slices(c, copy, tag):
            q_grouped[0, c] = keep.tile(
                [PART, PACK * ROUND_WIDTH[0]], BF16, name="q_grouped0_%d" % c, tag=tag, align_bytes=64
            )
            copy(
                out=q_grouped[0, c][:].rearrange("p (j i t) -> p j t i", i=PACK, t=PACK),
                in_=rounded[0, c][:].rearrange("p (t j i) -> p j t i", t=PACK, i=PACK),
            )

        def interleave_pairs(c):
            q_grouped[1, c] = keep.tile(
                [PART, PACK * ROUND_WIDTH[1]], BF16, name="q_grouped1_%d" % c, align_bytes=64
            )
            nc.vector.tensor_copy(
                out=q_grouped[1, c][:].bitcast(F32).rearrange("p (j u) -> p j u", u=2),
                in_=rounded[1, c][:].bitcast(F32).rearrange("p (u j) -> p j u", u=2),
            )

        def quantise_page(b, quarters, tag):
            name = "q%d_%d" % (b, quarters.start)
            codes = keep.tile([PART, len(quarters) * QUARTER], U32, name=name + "_codes", tag=tag, align_bytes=64)
            plane = keep.tile([PART, len(quarters) * QUARTER], U8, name=name + "_plane", align_bytes=64)
            for n, quarter in enumerate(quarters):
                c, j0 = divmod(quarter * QUARTER, ROUND_WIDTH[b])
                q_codes[b, quarter] = codes[:, n * QUARTER : (n + 1) * QUARTER]
                q_plane[b, quarter] = plane[:, n * QUARTER : (n + 1) * QUARTER]
                nc.vector.quantize_mx(
                    out=q_codes[b, quarter].bitcast(FP8X4), scales=q_plane[b, quarter],
                    in_=q_grouped[b, c][:, PACK * j0 : PACK * (j0 + QUARTER)],
                )

        first_response(0)
        for step in range(SLICES + ROUND_LAG):
            if step < SLICES:
                features(step)
                if step == 1:
                    fill_page(0)
                if step + 1 < SLICES:
                    first_response(step + 1)
                take_look(step)
                if step > 0:
                    fill_page(step)
                make_factor(step)
            if 1 <= step <= SLICES:
                write_page(step - 1)
            if step >= ROUND_LAG:
                round_page(step - ROUND_LAG)
            if step == 1:
                late_w1 = round_weight((1, 1), on_scalar, "pat1")
                late_w2 = round_weight((2, 1), on_scalar, "early_look0")
            if step == 2:
                quantise_weight((1, 1), late_w1, whole, "pat2")
                quantise_weight((2, 1), late_w2, whole, "early_look1")
            if step == PACK - 1 + ROUND_LAG:
                interleave_slices(0, nc.vector.tensor_copy, "pat6")
                interleave_slices(1, nc.scalar.copy, "pat5")
            if step == SLICES - 1:
                quantise_page(0, range(0, QUARTERS - 1), "factor0")
            if step == SLICES:
                quantise_page(0, range(QUARTERS - 1, QUARTERS), "look1")

        def reading_passes(bank, side, quarter, b):
            for n in range(2):
                rows = slice((2 * side + n) * PART, (2 * side + n + 1) * PART)
                nc.tensor.matmul_mx(
                    out=bank[:, n * QUARTER : (n + 1) * QUARTER],
                    lhsT=w4_sb[:, b, rows].bitcast(FP8X4), lhsT_scale=w4_plane[:, b, rows],
                    rhs=q_codes[b, quarter].bitcast(FP8X4), rhs_scale=q_plane[b, quarter],
                    start=(b == 0 and n == 0), stop=(b == GROUPS - 1 and n == 1),
                )

        sums = {}
        for quarter in range(QUARTERS):
            for side in range(2):
                sums[quarter, side] = take_bank()
                reading_passes(sums[quarter, side], side, quarter, 0)
        for quarter in range(QUARTERS):
            interleave_pairs(quarter)
            quantise_page(1, range(quarter, quarter + 1), "q_codes1_%d" % quarter)
            for side in range(2):
                reading_passes(sums[quarter, side], side, quarter, 1)
        out_rows = out.rearrange("(c p) j -> p c j", p=PART)
        for quarter in range(QUARTERS):
            for side in range(2):
                scores = keep.tile([PART, 2, QUARTER], F32, name="scores%d_%d" % (quarter, side))
                for n in range(2):
                    bias = beta_sb[:, 2 * side + n : 2 * side + n + 1]
                    tile_sums = sums[quarter, side][:, n * QUARTER : (n + 1) * QUARTER]
                    if side == 1 and quarter >= QUARTERS // 2:
                        nc.vector.tensor_scalar(
                            out=scores[:, n, :], in0=tile_sums, scalar1=bias, scalar2=None, op0=ALU.add
                        )
                    else:
                        nc.scalar.activation(out=scores[:, n, :], in_=tile_sums, func=ACT.Identity, bias=bias)
                nc.sync.dma_start(
                    out=out_rows[:, 2 * side : 2 * side + 2, quarter * QUARTER : (quarter + 1) * QUARTER],
                    in_=scores[:],
                )
